import numpy as np, ml_dtypes
CORES = [242,247,114,119]
N = 4
BF = ml_dtypes.bfloat16
V, CAP, LB, RO = 1792, 192, 4, 2
L = N * V
PL = (np.arange(N)[:, None] * V + np.arange(V)).reshape(N, 1, 1, V)
def draw(rng, size):
    s = (N, 8, 16, V)
    t = PL + 1 + (size * rng.random(s) * rng.random(s)).astype(np.int64)
    t = np.where(t > L, np.minimum(PL + 1 + ((L - PL) * rng.random(s)).astype(np.int64), L), t); z = rng.random(s)
    return np.where(z < 0.12, 0, np.where(z < 0.121, L, t))
def sizes(rng):
    a = np.array([V >> 6, V >> 5, V >> 4, V >> 3, V >> 3, V >> 2, V >> 1, 2 * V])[rng.permutation(8)]
    return (a[:, None] * np.exp2(2 * rng.random((8, 16)) - 1)).reshape(1, 8, 16, 1)
def perms(rng):
    return np.argsort(rng.random((N, 8, 16, LB)), axis=2)
def pack(t, rt):
    return {"ends": np.ascontiguousarray(t.reshape(N, 128, V)).astype(np.int32), "rights": np.ascontiguousarray(rt.reshape(N, 128, LB)).astype(np.int32)}
def setup_inputs(rng):
    return pack(draw(rng, sizes(rng)), perms(rng))
def setup_inputs_room(rng):
    t = draw(rng, np.full((1, 8, 16, 1), V >> 4)); p = np.arange(V)
    for r in range(N):
        for g in range(8):
            for b in range(LB):
                v = np.where((p == V - 1) | (rng.random(V) < 0.3), 0, r * V + p + 1 + ((V - 1 - p) * rng.random(V)).astype(np.int64))
                o = rng.permutation(V); k = 0
                for q in range(r + 1, N):
                    n = int(rng.choice(np.array([0, 1, CAP - 1, CAP, CAP + 1, 2 * CAP])))
                    if r == 0 and q == 1 and b == 0: n = (CAP, CAP + 1, 2 * CAP, CAP - 1, 1, 0, CAP, CAP + 1)[g]
                    x = rng.integers(0, V, n)
                    if n > 1: x[0] = 0; x[n - 1] = V - 1
                    v[o[k:k + n]] = q * V + x; k += n
                t[r, g, b] = v
    return pack(t, perms(rng))
def setup_inputs_alike(rng):
    t = draw(rng, sizes(rng)); p = PL.reshape(-1)
    for g in (0, 2, 4, 6):
        s = np.array([V, 1, 16, V // 4] * 4)
        if g: s = s[rng.permutation(16)]
        t[:, g] = np.minimum((PL[:, 0] // s[None, :, None] + 1) * s[None, :, None], L)
    for g in (1, 3):
        for a in range(16):
            cut = np.append(np.sort(rng.integers(1, L, 40)), L)
            t[:, g, a] = cut[np.searchsorted(cut, p, side="right")].reshape(N, V)
    rt = rng.integers(0, 16, (N, 8, 16, LB)); rt[:, 0] = np.arange(LB); rt[:, 2] = rng.choice(np.array([0, 15]), (N, 16, LB))
    return pack(t, rt)
def setup_inputs_fails(rng):
    t = draw(rng, sizes(rng)); rt = perms(rng); q = 1 + rng.permutation(7); h = V // 2; e = (N - 1) * V
    t[rng.integers(0, N), :, :LB] = 0
    t[:, 0, :LB] = 0; t[:, q[0], :LB] = 0; t[:, q[1], :LB] = L
    t[:, q[2]] = np.where(rng.random((N, 1, V)) < 0.6, 0, t[:, q[2]]); t[:, q[3], LB:] = 0
    b = int(rng.integers(0, LB))
    t[:, q[4], b] = np.where(rng.random((N, V)) < 0.1, L, 0); rt[:, q[4], b] = rng.integers(LB, 16, (N, LB))
    for s in (q[5], q[6]):
        t[:N - 1, s, :LB] = 0; t[N - 1, s, :, :h] = 0; t[N - 1, s, 0, :h] = e + h + rng.integers(0, h, h)
        for r in range(N - 1):
            o = rng.permutation(V)[:CAP]; t[r, s, 0, o] = e + rng.integers(0, h, CAP)
        rt[:N - 1, s, :, 0] = rng.integers(1, 15, (N - 1, 16))
    t[N - 1, q[6], 15, :h] = L; rt[:N - 1, q[6], 0, 0] = 15
    return pack(t, rt)
def setup_inputs_far(rng):
    t = draw(rng, np.full((1, 8, 16, 1), 8 * L))
    t[:, :, :LB] = np.where(rng.random((N, 8, LB, V)) < 0.85, 0, t[:, :, :LB])
    for r in range(N - 1):
        o = rng.permutation(8)
        for q in range(r + 1, N):
            b = int(rng.integers(1, LB)); v = np.where(rng.random(V) < 0.04, L, q * V + rng.integers(0, V, V))
            t[r, o[q], b] = v; t[r, o[q], 0] = np.where(rng.random(V) < 0.04, v, t[r, o[q], 0])
    t[:, :, :LB, 0] = L - 1; t[:, :, :LB, V - 1] = ((np.arange(N) + 1) * V)[:, None, None]
    return pack(t, perms(rng))
def setup_inputs_spread(rng):
    u = rng.random((N, 8, 16, V)) * np.sqrt(rng.random((N, 8, 1, V)))
    t = np.minimum(PL + np.maximum(np.exp2(np.log2(L - PL) * u).astype(np.int64), 1), L)
    t = np.where(rng.random(t.shape) < rng.random((N, 8, 1, 1)) * 0.3, 0, t)
    return pack(t, rng.integers(0, 16, (N, 8, 16, LB)))
def check_inputs(d):
    bad = []; a = np.asarray(d["ends"]).astype(np.int64); b = np.asarray(d["rights"])
    if not np.all((a == 0) | ((a > PL.reshape(N, 1, V)) & (a <= L))): bad.append("range of ends")
    if np.min(b) < 0 or np.max(b) > 15: bad.append("range of rights")
    return bad
def reference(ends, rights):
    m = np.ascontiguousarray(ends.astype(np.int64).reshape(N, 8, 16, V).transpose(1, 2, 0, 3)).reshape(8, 16, L)
    rt = rights.astype(np.int64).reshape(N, 8, 16, LB).transpose(1, 2, 0, 3)
    own = (np.arange(L) // V)[None, :]
    for rnd in range(RO):
        new = m
        for b in range(LB):
            t = m[:, b]; good = (t > 0) & (t < L); to = np.where(good, t // V, N)
            for q in range(1, N):
                far = (to == q) & (own < q)
                h = far.reshape(8, N, V).astype(np.int64); before = np.add.accumulate(h, axis=2) - h
                good = good & ~(far & (before.reshape(8, L) >= CAP))
            c = np.take_along_axis(m, np.where(good, t, 0)[:, None, :], 2)
            c = np.where(good[:, None, :], c, 0)
            c = np.take_along_axis(c.reshape(8, 16, N, V), rt[:, :, :, b:b + 1], 1).reshape(8, 16, L)
            new = np.maximum(new, c)
        m = new
    return {"y": np.ascontiguousarray(m.reshape(8, 16, N, V).transpose(2, 0, 1, 3)).reshape(N, 128, V).astype(np.float32)}

@@ -1,0 +1,404 @@
+from concourse.bass import DstId, RemoteDMATransfer
+from concourse.mybir import AluOpType as A, ActivationFunctionType as F
+
+V, NR, CAP = 1792, 4, 192
+L = NR * V
+PAD = 16
+WW = PAD + L + PAD
+C, B = 0.0122, 3584.0
+K = 1.0 / C
+MAGIC = 12582912.0
+OB = 192.0
+BIG = 8192.0
+
+LC = [448, 448, 448, 448]
+CH = [[[192, 416, 384, 544, 256], [448, 544, 448, 352]], [[320, 320, 416, 512, 224], [576, 544, 384, 288]],
+      [[352, 288, 384, 544, 224], [480, 544, 544, 224]], [[352, 384, 576, 288, 192], [448, 544, 640, 160]]]
+VS = [[[30, 40, 40, 0, 0, 0], [72, 6, 8, 4, 0, 0]], [[28, 28, 0, 44, 0, 0], [56, 26, 4, 0, 0, 0]],
+      [[24, 16, 16, 40, 0, 0], [56, 22, 16, 0, 0, 0]], [[44, 44, 20, 0, 0, 0], [80, 42, 0, 0, 0, 0]]]
+DEC = ["apaaavap", "ppppaavp", "aapaapap", "aaaaapap"]
+EO = ["va", "aa", "aa", "va"]
+EZ = "aa"
+PC = [[(0, 448), (448, 896), (896, 1344), (1344, 1792)], [(0, 512), (512, 1024), (1024, 1536), (1536, 1792)]]
+PO = [[(0, 896), (896, 1792)], [(0, 896), (896, 1536), (1536, 1792)]]
+DUP = [[], []]
+UP = [{"i1a": -3000, "i1v": 7000, "i1p": -56000, "da": 1000, "dp": -25000, "i0v": -15000, "g1a": 43000, "g0v": -71000, "g1v": -13000, "m0v": 8000, "dv": -2000, "m1v": 49000},
+      {"i1a": 21000, "i1v": 26000, "i1p": 8000, "da": -22000, "m0v": 38000, "g1a": -24000, "g0v": -6000, "i0v": -42000, "dp": -26000, "dv": 6000, "m1v": -1000},
+      {"i1a": -1000, "i1v": 3000, "i1p": 19000, "da": -12000, "i0v": 7000, "m0v": 5000, "dv": -16000, "dp": -7000, "g1a": -10000, "g0v": 27000, "m1v": 2000, "g1v": 3000},
+      {"i1a": 0, "i1v": 2000, "i1p": 9000, "da": -37000, "dp": 33000, "m0v": -1000, "i0v": 31000, "dv": -10000, "g0v": 1000, "g1a": -5000, "g1v": -24000}]
+NMAIN = 5
+NCH = 6
+NST = 8
+OW = 448 + 2 * NCH
+
+SCRATCH = {
+    "W0": ("sbuf", [128, WW], "bfloat16"), "W1": ("sbuf", [128, WW], "bfloat16"),
+    "G": ("sbuf", [128, 4 * V], "bfloat16"), "E": ("sbuf", [128, V], "int32"), "X": ("sbuf", [128, V], "float32"),
+    "Fo": ("sbuf", [128, V], "bfloat16"), "Ln": ("sbuf", [128, 896], "float32"),
+    "Ob": ("sbuf", [128, 2 * OW], "bfloat16"), "zb": ("sbuf", [128, 896], "bfloat16"),
+    "mb": ("sbuf", [128, 6 * OW], "bfloat16"), "cb": ("sbuf", [128, 6 * OW], "bfloat16"),
+    "sb": ("sbuf", [128, 6 * OW], "bfloat16"), "off": ("sbuf", [128, 896], "uint16"),
+    "rt": ("sbuf", [128, 4], "int32"), "a4": ("sbuf", [128, 4], "int32"), "a4m": ("sbuf", [128, 4], "int32"),
+    "rf": ("sbuf", [128, 4], "float32"),
+    "Ai": ("sbuf", [128, 128], "float32"), "Di": ("sbuf", [128, 128], "bfloat16"),
+    "S": ("sbuf", [128, 512], "bfloat16"), "Q": ("sbuf", [128, 512], "bfloat16"), "P": ("sbuf", [128, 512], "bfloat16"),
+    "Ip": ("sbuf", [128, 128], "bfloat16"), "Im": ("sbuf", [128, 128], "bfloat16"), "Ik": ("sbuf", [128, 128], "float32"),
+    "n1": ("sbuf", [128, 128], "bfloat16"), "n2": ("sbuf", [128, 128], "bfloat16"),
+    "NB": ("sbuf", [128, 128], "bfloat16"), "NT": ("sbuf", [128, 128], "bfloat16"),
+    "z0": ("sbuf", [128, 16], "float32"),
+    "pR": ("psum", [128, 512], "float32"), "pU0": ("psum", [128, 512], "float32"), "pU1": ("psum", [128, 512], "float32"),
+}
+for _i in range(NMAIN):
+    SCRATCH["pm%d" % _i] = ("psum", [128, 512], "float32")
+
+SEMAPHORES = ["cv", "ca", "cp", "cg", "sent", "a0", "a1", "lr"]
+SEMAPHORES += ["ld%d" % i for i in range(6)] + ["st%d" % i for i in range(NST)]
+SEMAPHORES += ["f%d_%d_%d" % (rd, s, p) for rd in range(2) for s in (2, 3) for p in range(6)]
+
+EST = {"cy": 1.04, "pe": 0.55, "lat": 110.0, "fix": 30.0, "ga": 1.56, "far": 7.5, "near": 11.0, "first": 2000.0, "win": 150.0}
+CSEM = {"v": "cv", "a": "ca", "p": "cp", "g": "cg"}
+
+
+def starts(ws):
+    out, x = [], 0
+    for w in ws:
+        out.append((x, w))
+        x += w
+    return out
+
+
+def bits(m):
+    return bin(m).count("1")
+
+
+def build(r, g, T, topo, arr):
+    ops = []
+    lab = [""]
+    core = T.cores[r]
+    qs = list(range(r + 1, NR))
+    nq = len(qs)
+    own = PAD + r * V
+    W = [lambda: T.W0, lambda: T.W1]
+    CY, PE, FIX, GA = EST["cy"], EST["pe"], EST["fix"], EST["ga"]
+
+    def op(eng, dur, deps, fn, ext=(), kind="c", sem=None, tail=0.0, lat=0.0, send=None):
+        o = {"e": eng, "d": dur, "deps": [x for x in deps if x is not None], "fn": fn, "ext": list(ext), "k": kind,
+             "sem": sem, "tail": tail, "lat": lat, "send": send, "i": len(ops), "up": UP[r].get(lab[0] + eng, 0.0)}
+        ops.append(o)
+        return o
+
+    def vc(n):
+        return max(64.0, n) * CY + FIX
+
+    def V1(n, deps, fn, **kw):
+        return op("v", vc(n), deps, lambda: [fn()], **kw)
+
+    def A1(n, deps, fn, **kw):
+        return op("a", vc(n) + 20 + kw.pop("extra", 0), deps, lambda: [fn()], **kw)
+
+    def G1(n, deps, fn):
+        return op("g", 170 + 2 * n * CY, deps, lambda: [fn()])
+
+    def over(lst, lo, hi):
+        return [o for (a, b, o) in lst if a < hi and lo < b]
+
+    lds = []
+    tl = 1900.0
+    for j, (x0, w) in enumerate(starts(LC)):
+        tl += 128 * w * 4 / 220.0
+        q = "s" if j % 2 == 0 else "a"
+        lds.append(op(q, 60, [], lambda x0=x0, w=w, q=q: [(g.sync if q == "s" else g.scalar).dma_start(T.E[:, x0:x0 + w], T.ends[:, x0:x0 + w])],
+                      kind="d", sem="ld%d" % j, lat=tl, tail=1e6 - 1000 * j))
+    ldr = op("s", 60, [], lambda: [g.sync.dma_start(T.rt[:], T.rights[:])], kind="d", sem="lr", lat=tl, tail=9e5)
+
+    gA = G1(128, [], lambda: g.iota(T.Ai[:], [[-16, 8], [-1, 4], [-200, 4]], 0, 1, allow_small_or_imprecise_dtypes=True))
+    gD = G1(128, [], lambda: g.iota(T.Di[:], [[1, 128]], 0, -1, allow_small_or_imprecise_dtypes=True))
+    g4 = G1(4, [], lambda: g.iota(T.a4[:], [[0, 4]], 0, 1))
+    cS = [V1(128, [gA], lambda i=i: g.vector.tensor_scalar(T.S[:, 128 * i:128 * i + 128], T.Ai[:], -200.0 * i, None, A.is_equal)) for i in range(4)]
+    cK = V1(128, [gD], lambda: g.vector.tensor_scalar(T.Ik[:], T.Di[:], 0.0, K, A.is_equal, A.mult))
+    cM = cP = cO = cNB = cNT = None
+    if nq:
+        cM = V1(64, [gD], lambda: g.vector.tensor_scalar(T.Im[:], T.Di[:], 0.0, -BIG, A.is_equal, A.mult))
+        cP = V1(64, [gD], lambda: g.vector.tensor_scalar(T.Ip[:], T.Di[:], 0.0, BIG, A.is_equal, A.mult))
+        cO = V1(OW, [], lambda: g.vector.memset(T.Ob[:], 0.0))
+        c1 = V1(64, [], lambda: g.vector.memset(T.n1[:], -1.0))
+        c2 = G1(128, [c1], lambda: g.affine_select(T.n2[:], T.n1[:], [[-4, 32], [0, 4]], A.is_ge, 0.0, 0, 1))
+        cNT = G1(128, [c2], lambda: g.affine_select(T.NT[:], T.n2[:], [[1, 128]], A.is_gt, 0.0, 0, -1))
+        cNB = G1(128, [c2], lambda: g.affine_select(T.NB[:], T.n2[:], [[4, 32], [0, 4]], A.is_ge, 0.0, 3, -1))
+    c4 = V1(4, [g4], lambda: g.vector.tensor_scalar(T.a4m[:], T.a4[:], 15, None, A.bitwise_and))
+    cf = V1(8, [c4, ldr], lambda: g.vector.tensor_tensor(T.rf[:], T.rt[:], T.a4m[:], A.subtract))
+    cQ = [V1(64, [cf, gD], lambda b=b: g.vector.tensor_scalar(T.Q[:, 128 * b:128 * b + 128], T.Di[:], T.rf[:, b:b + 1], None, A.is_equal)) for b in range(4)]
+    cT = V1(256, cQ, lambda: g.vector.transpose(T.P[:], T.Q[:]))
+    cz = V1(16, [], lambda: g.vector.memset(T.z0[:], 0.0), tail=1e5)
+    zero = [[], []]
+    for rd in range(2):
+        for col in (r * V, PAD + L):
+            zero[rd].append(A1(16, [cz], lambda rd=rd, col=col: g.scalar.activation(W[rd]()[:, col:col + PAD], T.z0[:], F.Exp, bias=-C * B, scale=C),
+                               extra=1300 if (rd == 0 and col == r * V) else 0, tail=1e5 if (rd == 0 and col == r * V) else 5e4))
+
+    wr = [[], []]
+    for j, (x0, w) in enumerate(starts(LC)):
+        cv = V1(w, [lds[j]], lambda x0=x0, w=w: g.vector.tensor_copy(T.X[:, x0:x0 + w], T.E[:, x0:x0 + w]))
+        wr[0].append((x0, x0 + w, A1(w, [cv], lambda x0=x0, w=w: g.scalar.activation(T.W0[:, own + x0:own + x0 + w], T.X[:, x0:x0 + w], F.Exp, bias=-C * B, scale=C))))
+    allexp = [o for (_, _, o) in wr[0]] + zero[0] + zero[1]
+
+    st = {"R": None, "U": [None, None], "M": [None] * NMAIN, "nb": 0, "nu": 0, "ln": 0}
+
+    def index(rd):
+        fins, scans = [], []
+        lab[0] = "i%d" % rd
+        for c, (x0, w) in enumerate(starts(CH[r][rd])):
+            n, k0 = w // 4, x0 // 4
+            ns = n + 2
+            lc = 448 * rd + k0
+            rel = op("p", 4 * max(64, n) * PE + FIX, over(wr[rd], x0, x0 + w) + cS + [st["R"]],
+                     lambda rd=rd, x0=x0, n=n: [g.tensor.matmul(T.pR[:, 0:n], T.S[:, 128 * i:128 * i + 128], W[rd]()[:, own + x0 + n * i:own + x0 + n * i + n], i == 0, i == 3) for i in range(4)])
+            ln = A1(n, [rel] + allexp, lambda lc=lc, n=n: g.scalar.activation(T.Ln[:, lc:lc + n], T.pR[:, 0:n], F.Ln), extra=1500 if st["ln"] == 0 else 0)
+            st["ln"] = 1
+            st["R"] = ln
+            u = st["nu"] % 2
+            st["nu"] += 1
+            pu = "pU%d" % u
+            terms, deps = [], [ln, cK, st["U"][u]]
+            if nq:
+                ob = OW * rd + k0 + 2 * c
+                mb = nq * ob
+                sc0, bi0 = K / V, (B + 0.5) / V - 0.5 + OB
+                if EO[r][rd] == "v":
+                    o1 = V1(n, [ln, cO], lambda lc=lc, n=n, ob=ob: g.vector.tensor_scalar(T.Ob[:, ob + 2:ob + 2 + n], T.Ln[:, lc:lc + n], sc0, bi0, A.mult, A.add))
+                else:
+                    o1 = A1(n, [ln, cO], lambda lc=lc, n=n, ob=ob: g.scalar.activation(T.Ob[:, ob + 2:ob + 2 + n], T.Ln[:, lc:lc + n], F.Identity, bias=bi0, scale=sc0))
+                ms = [V1(ns / 2, [o1], lambda ob=ob, ns=ns, a=mb + j * ns, q=q: g.vector.tensor_scalar(T.mb[:, a:a + ns], T.Ob[:, ob:ob + ns], OB + q, None, A.is_equal)) for j, q in enumerate(qs)]
+                sc = [V1(ns / 2, [ms[j]], lambda a=mb + j * ns, ns=ns: g.vector.tensor_tensor_scan(T.cb[:, a:a + ns], T.mb[:, a:a + ns], T.mb[:, a:a + ns], 0.0, A.add, A.max)) for j in range(nq)]
+                scans.append((mb, ns, sc))
+                ca = op("p", 64 * len(scans) * PE + FIX, [x for (_, _, s) in scans for x in s] + [cNT, cNB, st["U"][u]],
+                        lambda sl=[(a, b) for (a, b, _) in scans], pu=pu: [g.tensor.matmul(T[pu][:, 0:nq], (T.NT if j == len(sl) - 1 else T.NB)[:], T.cb[:, a + b - 1:a + nq * b:b], j == 0, j == len(sl) - 1) for j, (a, b) in enumerate(sl)])
+                sat = [V1(ns / 2, [ca], lambda a=mb + j * ns, ns=ns, j=j, pu=pu: g.vector.tensor_scalar(T.sb[:, a:a + ns], T.cb[:, a:a + ns], -float(CAP), T[pu][:, j:j + 1], A.add, A.max)) for j in range(nq)]
+                deps += sat + [cM, cP]
+                for j in range(nq):
+                    terms += [("Im", "sb", mb + j * ns + 2), ("Ip", "sb", mb + j * ns + 1)]
+            if r == 0:
+                if EZ[rd] == "v":
+                    deps.append(V1(n, [ln], lambda lc=lc, n=n: g.vector.tensor_scalar(T.zb[:, lc:lc + n], T.Ln[:, lc:lc + n], C * (0.5 - B), None, A.is_lt)))
+                else:
+                    deps.append(A1(n, [ln], lambda lc=lc, n=n: g.scalar.activation(T.zb[:, lc:lc + n], T.Ln[:, lc:lc + n], F.Relu, bias=800.0 * C * (0.5 - B), scale=-800.0)))
+                terms.append(("Im", "zb", lc))
+            terms.append(("Ik", "Ln", lc))
+            um = op("p", (len(terms) + 3) * max(64, n) * PE + FIX, deps,
+                    lambda terms=terms, n=n, pu=pu: [g.tensor.matmul(T[pu][:, 8:8 + n], T[a][:], T[b][:, x:x + n], j == 0, j == len(terms) - 1) for j, (a, b, x) in enumerate(terms)])
+            fin = V1(n, [um], lambda lc=lc, n=n, pu=pu: g.vector.tensor_scalar(T.off[:, lc:lc + n], T[pu][:, 8:8 + n], MAGIC + B + PAD - r * V, MAGIC, A.add, A.subtract))
+            st["U"][u] = fin
+            fins.append(fin)
+        return fins
+
+    def arrivals(rd):
+        if r == 1:
+            names = ["f%d_%d_%d" % (rd, s, p) for s in (2, 3) for p in range(len(PC[rd]))]
+        elif r == 3:
+            names = []
+        else:
+            names = ["a%d" % rd]
+        return [(s, arr[(r, s)][1], arr[(r, s)][0]) for s in names]
+
+    def main(rd, fins):
+        res = []
+        tbl = [o for (_, _, o) in wr[rd]] + zero[rd]
+        for c, (x0, w) in enumerate(starts(CH[r][rd])):
+            n, lc = w // 4, 448 * rd + x0 // 4
+            kv = VS[r][rd][c]
+            gs = []
+            lab[0] = "g%d" % rd
+
+            def win(rd, a, b):
+                return W[rd]()[:, r * V:WW].indirect(T.off[:, a:b])
+            if kv:
+                gs.append(V1(16 * kv * GA, tbl + [fins[c]], lambda rd=rd, lc=lc, kv=kv, x0=x0: g.vector.tensor_copy(T.G[:, 4 * x0:4 * x0 + 16 * kv], win(rd, lc, lc + kv)), ext=arrivals(rd)))
+            if kv < n:
+                gs.append(A1(16 * (n - kv) * GA, tbl + [fins[c]], lambda rd=rd, lc=lc, kv=kv, x0=x0, n=n: g.scalar.activation(T.G[:, 4 * x0 + 16 * kv:4 * x0 + 16 * n], win(rd, lc + kv, lc + n), F.Copy), ext=arrivals(rd)))
+            lab[0] = "m%d" % rd
+            parts = [(0, 4)] if w <= 512 else [(0, 2), (2, 4)]
+            prev = [None] * len(parts)
+            for b in range(4):
+                for h, (i0, i1) in enumerate(parts):
+                    bk = st["nb"] % NMAIN
+                    st["nb"] += 1
+                    pm = "pm%d" % bk
+                    mm = op("p", (i1 - i0) * max(64, n) * PE + FIX, gs + [cT, st["M"][bk]],
+                            lambda pm=pm, b=b, n=n, x0=x0, i0=i0, i1=i1: [g.tensor.matmul(T[pm][:, n * (i - i0):n * (i - i0) + n], T.P[:, 128 * b:128 * b + 128], T.G[:, 4 * x0 + 4 * b + i:4 * x0 + 16 * n:16], True, True) for i in range(i0, i1)])
+
+                    def mx(pm=pm, b=b, xa=x0 + n * i0, xb=x0 + n * i1, rd=rd):
+                        dst = T.W1[:, own + xa:own + xb] if rd == 0 else T.Fo[:, xa:xb]
+                        src = W[rd]()[:, own + xa:own + xb] if b == 0 else dst
+                        return g.vector.tensor_tensor(dst, T[pm][:, 0:xb - xa], src, A.max)
+                    prev[h] = V1(n * (i1 - i0), [mm, prev[h]], mx)
+                    st["M"][bk] = prev[h]
+            for h, (i0, i1) in enumerate(parts):
+                res.append((x0 + n * i0, x0 + n * i1, prev[h]))
+        return res
+
+    def sends(rd):
+        lab[0] = "s"
+
+        def tr(dst, src, a, b, mask, sem):
+            rid, pid = topo.addr(T.cores[dst], core)
+            ap = W[rd]()[:, PAD + src * V + a:PAD + src * V + b]
+            return RemoteDMATransfer(dst_ids=[DstId(rid=rid, pnc=pid)], dma_engine_mask=mask, remote_sem=T.sem[sem], src=ap, dst=ap)
+
+        def snd(lst, deps, ext, tail):
+            op("g", 400, deps, lambda lst=lst: [g.remote_dma_fused([tr(*x) for x in lst], local_sem=T.sem.sent)], ext=ext, kind="r", send=lst, tail=tail)
+        rest = 14000.0 * (2 - rd) + 4000
+        if r >= 2:
+            far = topo.mask(core, T.cores[1])
+            en = topo.engines(core, T.cores[1])
+            lo = sum(1 << e for e in en[:len(en) // 2])
+            for p, (a, b) in enumerate(PC[rd]):
+                if p in DUP[rd]:
+                    lst = [(1, r, a, b, lo, "f%d_%d_%d" % (rd, r, p)), (0, r, a, b, far & ~lo, "a%d" % rd)]
+                else:
+                    lst = [(1, r, a, b, far, "f%d_%d_%d" % (rd, r, p))]
+                if r == 3:
+                    lst.append((2, r, a, b, topo.mask(core, T.cores[2]) & ~far, "a%d" % rd))
+                snd(lst, over(wr[rd], a, b), [], rest + 9000 - 2000 * p)
+        if r == 1:
+            full = topo.mask(core, T.cores[0])
+            en = topo.engines(core, T.cores[0])
+            lo = sum(1 << e for e in en[:len(en) // 2])
+            for p, (a, b) in enumerate(PO[rd]):
+                snd([(0, 1, a, b, full, "a%d" % rd)], over(wr[rd], a, b), [], rest + 3000 - 500 * p)
+            for p, (a, b) in enumerate(PC[rd]):
+                if p in DUP[rd]:
+                    continue
+                ext = [(s, arr[(r, s)][1], arr[(r, s)][0]) for s in ("f%d_2_%d" % (rd, p), "f%d_3_%d" % (rd, p))]
+                snd([(0, 2, a, b, lo, "a%d" % rd), (0, 3, a, b, full & ~lo, "a%d" % rd)], [], ext, rest + 3000 - 500 * p)
+
+    sends(0)
+    f0 = index(0)
+    wr[1] = main(0, f0)
+    sends(1)
+    f1 = index(1)
+    last = main(1, f1)
+    lab[0] = "d"
+    for c, (x0, x1, o) in enumerate(last):
+        w = x1 - x0
+        ln = A1(w, [o], lambda x0=x0, x1=x1: g.scalar.activation(T.X[:, x0:x1], T.Fo[:, x0:x1], F.Ln))
+        if DEC[r][c] == "p":
+            u = st["nu"] % 2
+            st["nu"] += 1
+            d1 = op("p", 4 * w * PE + FIX, [ln, st["U"][u]], lambda x0=x0, x1=x1, u=u: [g.tensor.matmul(T["pU%d" % u][:, 0:x1 - x0], T.Ik[:], T.X[:, x0:x1], True, True)])
+            d2 = V1(w, [d1], lambda x0=x0, x1=x1, u=u: g.vector.tensor_scalar(T.X[:, x0:x1], T["pU%d" % u][:, 0:x1 - x0], MAGIC + B, MAGIC, A.add, A.subtract))
+            st["U"][u] = d2
+        else:
+            if DEC[r][c] == "a":
+                d1 = A1(w, [ln], lambda x0=x0, x1=x1: g.scalar.activation(T.X[:, x0:x1], T.X[:, x0:x1], F.Identity, bias=MAGIC + B, scale=K))
+            else:
+                d1 = V1(w, [ln], lambda x0=x0, x1=x1: g.vector.tensor_scalar(T.X[:, x0:x1], T.X[:, x0:x1], K, MAGIC + B, A.mult, A.add))
+            d2 = V1(w, [d1], lambda x0=x0, x1=x1: g.vector.tensor_scalar(T.X[:, x0:x1], T.X[:, x0:x1], MAGIC, None, A.subtract))
+        op("s", 60, [d2], lambda x0=x0, x1=x1: [g.sync.dma_start(T.y[:, x0:x1], T.X[:, x0:x1])], kind="d", sem="st%d" % c, lat=1900 + 128 * w * 4 / 220.0)
+    return ops
+
+
+def order(ops):
+    LAT = EST["lat"]
+    users = [[] for _ in ops]
+    for o in ops:
+        for d in o["deps"]:
+            users[d["i"]].append(o)
+    for o in reversed(ops):
+        o["pr"] = o["d"] + o["lat"] + max([o["tail"]] + [u["pr"] + LAT for u in users[o["i"]]])
+    for o in ops:
+        o["pr"] += o["up"]
+    free = {}
+    left = [len(o["deps"]) for o in ops]
+    cand = []
+
+    def enter(o):
+        o["rdy"] = max([0.0] + [d["end"] + LAT for d in o["deps"]] + [x[2] + LAT for x in o["ext"]])
+        cand.append(o)
+    for o in ops:
+        if not o["deps"]:
+            enter(o)
+    seq = []
+    while cand:
+        for o in cand:
+            o["t"] = max(free.get(o["e"], 0.0), o["rdy"])
+        first = min(cand, key=lambda o: (o["t"], -o["pr"]))
+        o = max([x for x in cand if x["e"] == first["e"] and x["t"] <= first["t"] + EST["win"]], key=lambda x: x["pr"])
+        cand[:] = [x for x in cand if x["i"] != o["i"]]
+        free[o["e"]] = o["t"] + o["d"]
+        o["end"] = o["t"] + o["d"] + o["lat"]
+        seq.append(o)
+        for u in users[o["i"]]:
+            left[u["i"]] -= 1
+            if left[u["i"]] == 0:
+                enter(u)
+    return seq
+
+
+def landings(r, seq, T, topo, arr):
+    busy, first = {}, EST["first"]
+    for o in seq:
+        if o["k"] != "r":
+            continue
+        for (dst, src, a, b, mask, sem) in o["send"]:
+            far = topo.host(T.cores[dst]) != topo.host(T.cores[r])
+            rate = (EST["far"] if far else EST["near"]) * bits(mask)
+            t0 = o["t"] + o["d"] + first + 1500.0
+            es = [e for e in topo.engines(T.cores[r], T.cores[dst]) if mask >> e & 1]
+            t1 = max([t0] + [busy.get(e, 0.0) for e in es]) + 256.0 * (b - a) / rate
+            for e in es:
+                busy[e] = t1
+            old = arr.get((dst, sem), (0.0, 0))
+            arr[(dst, sem)] = (max(old[0], t1 + 500.0), old[1] + bits(mask))
+        first = 0.0
+
+
+def plan(rank, g, T, topo):
+    arr = {}
+    for r in range(NR - 1, rank - 1, -1):
+        seq = order(build(r, g, T, topo, arr))
+        landings(r, seq, T, topo, arr)
+    return seq
+
+
+def rank_program(g, core, T, topo):
+    rank = T.rank_of(core)
+    if rank is None:
+        return
+    seq = plan(rank, g, T, topo)
+    Q = {"v": g.vector, "a": g.scalar, "p": g.tensor, "s": g.sync, "g": g}
+    cnt = {e: 0 for e in CSEM}
+    seen = {}
+    sent = 0
+    stores = []
+    for o in seq:
+        e = o["e"]
+        need = {}
+        for d in o["deps"]:
+            s, v = d["sig"]
+            need[s] = max(need.get(s, 0), v)
+        for (s, v, _) in o["ext"]:
+            need[s] = max(need.get(s, 0), v)
+        for s, v in need.items():
+            if seen.get((e, s), 0) < v:
+                Q[e].wait_ge(T.sem[s], v)
+                seen[(e, s)] = v
+        ins = o["fn"]()
+        if o["k"] == "c":
+            for x in ins:
+                x.then_inc(T.sem[CSEM[e]], 1)
+                cnt[e] += 1
+            o["sig"] = (CSEM[e], cnt[e])
+        elif o["k"] == "d":
+            ins[0].then_inc(T.sem[o["sem"]], 16)
+            o["sig"] = (o["sem"], 16)
+            if o["sem"].startswith("st"):
+                stores.append(o["sem"])
+        else:
+            sent += sum(bits(x[4]) for x in o["send"])
+    if sent:
+        g.wait_ge(T.sem.sent, sent)
+    for e in CSEM:
+        if max([0] + [v for (k, v) in seen.items() if k[1] == CSEM[e]]) < cnt[e]:
+            g.wait_ge(T.sem[CSEM[e]], cnt[e])
+    for s in stores:
+        g.sync.wait_ge(T.sem[s], 16)

@@ -3,66 +3,61 @@ from concourse.mybir import AluOpType as A, ActivationFunctionType as F
 
 V, NR, CAP = 1792, 4, 192
 L = NR * V
-PAD = 16
-WW = PAD + L + PAD
+GAP = 16
+TW = V + GAP
+WW = NR * TW + 32
 C, B = 0.0122, 3584.0
 K = 1.0 / C
 MAGIC = 12582912.0
+ROOT = 3072.0
 OB = 192.0
 BIG = 8192.0
+TOP = 200.0
+Q4 = V // 4
 
-LC = [448, 448, 448, 448]
-CH = [[[192, 416, 384, 544, 256], [448, 544, 448, 352]], [[320, 320, 416, 512, 224], [576, 544, 384, 288]],
-      [[352, 288, 384, 544, 224], [480, 544, 544, 224]], [[352, 384, 576, 288, 192], [448, 544, 640, 160]]]
-VS = [[[30, 40, 40, 0, 0, 0], [72, 6, 8, 4, 0, 0]], [[28, 28, 0, 44, 0, 0], [56, 26, 4, 0, 0, 0]],
-      [[24, 16, 16, 40, 0, 0], [56, 22, 16, 0, 0, 0]], [[44, 44, 20, 0, 0, 0], [80, 42, 0, 0, 0, 0]]]
-DEC = ["apaaavap", "ppppaavp", "aapaapap", "aaaaapap"]
-EO = ["va", "aa", "aa", "va"]
-EZ = "aa"
-PC = [[(0, 448), (448, 896), (896, 1344), (1344, 1792)], [(0, 512), (512, 1024), (1024, 1536), (1536, 1792)]]
-PO = [[(0, 896), (896, 1792)], [(0, 896), (896, 1536), (1536, 1792)]]
-DUP = [[], []]
-UP = [{"i1a": -3000, "i1v": 7000, "i1p": -56000, "da": 1000, "dp": -25000, "i0v": -15000, "g1a": 43000, "g0v": -71000, "g1v": -13000, "m0v": 8000, "dv": -2000, "m1v": 49000},
-      {"i1a": 21000, "i1v": 26000, "i1p": 8000, "da": -22000, "m0v": 38000, "g1a": -24000, "g0v": -6000, "i0v": -42000, "dp": -26000, "dv": 6000, "m1v": -1000},
-      {"i1a": -1000, "i1v": 3000, "i1p": 19000, "da": -12000, "i0v": 7000, "m0v": 5000, "dv": -16000, "dp": -7000, "g1a": -10000, "g0v": 27000, "m1v": 2000, "g1v": 3000},
-      {"i1a": 0, "i1v": 2000, "i1p": 9000, "da": -37000, "dp": 33000, "m0v": -1000, "i0v": 31000, "dv": -10000, "g0v": 1000, "g1a": -5000, "g1v": -24000}]
-NMAIN = 5
-NCH = 6
-NST = 8
-OW = 448 + 2 * NCH
+PAR = {"LC":[96,320,320,608,448],"IC":[[[608,576,288,320],[480,352,416,544]],[[928,864],[288,288,672,544]],[[448,384,384,576],[384,352,224,288,544]],[[576,384,832],[672,192,192,352,352,32]]],"PT":[[[[384,176],[480,80],[320,48],[416,48],[192,64]],[[416,224],[448,144],[352,112],[192,64]]],[[[448,272],[448,32],[416,48],[320,0],[160,48]],[[352,128],[480,224],[-160,16,0],[-224,48,0],[448,80],[128,128]]],[[[224,128],[96,80],[512,80],[512,80],[288,112],[160,0]],[[160,160],[256,0],[352,176],[256,80],[-160,0,1],[-224,32,1],[256,16],[160,64]]],[[[96,96],[96,0],[64,0],[256,80],[320,96],[480,112],[480,0]],[[32,32],[448,160],[384,0],[128,64],[-352,32,2],[384,128],[96,96],[256,0],[64,0]]]],"EI":[["aav","aaa"],["vva","aav"],["vvv","aav"],["vvv","avv"]],"PC":[[[96,608,640,448],[96,608,640,448]],[[320,512,512,288,160],[544,256,224,768]]],"DUP":[[0,0],[2,3]],"PO":[[[],[800,800,192]],[[64,448,1280],[832,416,384,160]]],"ED":["axyxwvvvvv","xvayyxvvvv","wvavxwwyvv","avxxwayxwa"],"FO":[0,1,0,1],"RAW":[2,1,1,9],"PASS":1,"MIX":0.5,"QW":0.9,"LN":["gv","ga",None],"NAUX":3,"SPLIT":300,"UP":[{"i1a":-1000,"i1v":9000,"i1p":9000,"j1p":8000,"sndg":-3000,"m0p":8000,"exa":-8000,"j0p":-8000,"g0v":3000,"v":-8000},{"i1a":9000,"i1v":9000,"i1p":9000,"j1v":3000,"g0v":1000,"dv":-3000,"g1a":1000,"dp":-1000,"j0a":1000},{"i1a":8000,"g0a":-8000,"j1v":-8000,"exa":8000,"i1p":-8000,"i1v":-8000,"sndg":8000,"cvv":-3000,"j0a":8000,"j1a":8000,"i0v":3000},{"i1a":8000,"i0a":30000,"m1v":30000,"i1v":8000,"g1a":-3000,"j0v":-1000,"dv":8000,"sndg":1000,"m0v":3000,"j0p":-3000,"j1p":-8000,"i0p":-1000}],"WIN":{"a":200,"v":30,"p":30,"g":200,"s":500},"HOP":[700,1000,700,1000],"HUB":[[1,1],[0,1]]}
+HM = 1024
+NP = 8
 
 SCRATCH = {
     "W0": ("sbuf", [128, WW], "bfloat16"), "W1": ("sbuf", [128, WW], "bfloat16"),
-    "G": ("sbuf", [128, 4 * V], "bfloat16"), "E": ("sbuf", [128, V], "int32"), "X": ("sbuf", [128, V], "float32"),
-    "Fo": ("sbuf", [128, V], "bfloat16"), "Ln": ("sbuf", [128, 896], "float32"),
-    "Ob": ("sbuf", [128, 2 * OW], "bfloat16"), "zb": ("sbuf", [128, 896], "bfloat16"),
-    "mb": ("sbuf", [128, 6 * OW], "bfloat16"), "cb": ("sbuf", [128, 6 * OW], "bfloat16"),
-    "sb": ("sbuf", [128, 6 * OW], "bfloat16"), "off": ("sbuf", [128, 896], "uint16"),
-    "rt": ("sbuf", [128, 4], "int32"), "a4": ("sbuf", [128, 4], "int32"), "a4m": ("sbuf", [128, 4], "int32"),
+    "G": ("sbuf", [128, 4 * V], "bfloat16"),
+    "E": ("sbuf", [128, V], "int32"), "X": ("sbuf", [128, V], "float32"), "Yl": ("sbuf", [128, HM], "float32"),
+    "F": ("sbuf", [128, V], "bfloat16"), "Ln": ("sbuf", [128, 2 * Q4], "float32"),
+    "Ob": ("sbuf", [128, 2 * Q4], "bfloat16"), "zb": ("sbuf", [128, 2 * Q4], "bfloat16"),
+    "mb": ("sbuf", [128, 6 * Q4], "bfloat16"), "cb": ("sbuf", [128, 6 * Q4], "bfloat16"),
+    "fb": ("sbuf", [128, 6 * Q4], "bfloat16"), "top": ("sbuf", [128, Q4], "bfloat16"),
+    "off": ("sbuf", [128, 2 * Q4], "uint16"),
+    "rt": ("sbuf", [128, 4], "int32"), "a4": ("sbuf", [128, 4], "int32"), "a15": ("sbuf", [128, 4], "int32"),
+    "a12": ("sbuf", [128, 4], "int32"), "f12": ("sbuf", [128, 4], "float32"), "row": ("sbuf", [128, 4], "float32"),
     "rf": ("sbuf", [128, 4], "float32"),
-    "Ai": ("sbuf", [128, 128], "float32"), "Di": ("sbuf", [128, 128], "bfloat16"),
-    "S": ("sbuf", [128, 512], "bfloat16"), "Q": ("sbuf", [128, 512], "bfloat16"), "P": ("sbuf", [128, 512], "bfloat16"),
-    "Ip": ("sbuf", [128, 128], "bfloat16"), "Im": ("sbuf", [128, 128], "bfloat16"), "Ik": ("sbuf", [128, 128], "float32"),
-    "n1": ("sbuf", [128, 128], "bfloat16"), "n2": ("sbuf", [128, 128], "bfloat16"),
-    "NB": ("sbuf", [128, 128], "bfloat16"), "NT": ("sbuf", [128, 128], "bfloat16"),
-    "z0": ("sbuf", [128, 16], "float32"),
-    "pR": ("psum", [128, 512], "float32"), "pU0": ("psum", [128, 512], "float32"), "pU1": ("psum", [128, 512], "float32"),
+    "A2": ("sbuf", [128, 128], "bfloat16"), "Di": ("sbuf", [128, 128], "bfloat16"),
+    "S": ("sbuf", [128, 512], "bfloat16"), "S4": ("sbuf", [128, 512], "float32"),
+    "Q": ("sbuf", [128, 512], "bfloat16"), "P": ("sbuf", [128, 512], "bfloat16"),
+    "Ig": ("sbuf", [128, 128], "bfloat16"), "Im": ("sbuf", [128, 128], "bfloat16"), "Ik": ("sbuf", [128, 128], "float32"),
+    "NB": ("sbuf", [128, 128], "bfloat16"), "NN": ("sbuf", [128, 128], "bfloat16"), "NU": ("sbuf", [128, 128], "bfloat16"),
+    "ND": ("sbuf", [128, 128], "bfloat16"), "z0": ("sbuf", [128, 16], "float32"), "rt2": ("sbuf", [128, 512], "bfloat16"),
 }
-for _i in range(NMAIN):
-    SCRATCH["pm%d" % _i] = ("psum", [128, 512], "float32")
+for _i in range(8):
+    SCRATCH["ps%d" % _i] = ("psum", [128, 512], "float32")
+for _i in (1, 2):
+    SCRATCH.update({"Gh%d" % _i: ("sbuf", [128, 4 * HM], "bfloat16"), "Ph%d" % _i: ("sbuf", [128, 512], "bfloat16"),
+                    "Fh%d" % _i: ("sbuf", [128, HM], "bfloat16"), "Xh%d" % _i: ("sbuf", [128, HM], "float32"),
+                    "offh%d" % _i: ("sbuf", [128, Q4], "uint16")})
 
-SEMAPHORES = ["cv", "ca", "cp", "cg", "sent", "a0", "a1", "lr"]
-SEMAPHORES += ["ld%d" % i for i in range(6)] + ["st%d" % i for i in range(NST)]
-SEMAPHORES += ["f%d_%d_%d" % (rd, s, p) for rd in range(2) for s in (2, 3) for p in range(6)]
+SEMAPHORES = ["cv", "ca", "cp", "cg", "sent", "a0", "a1", "lr", "h0", "h1", "h2", "t0", "t1", "t2"]
+SEMAPHORES += ["ld%d" % i for i in range(NP)] + ["st%d" % i for i in range(2 * NP)] + ["y%d" % i for i in range(NP)]
+SEMAPHORES += ["f%d_%d_%d" % (rd, s, p) for rd in range(2) for s in (2, 3) for p in range(NP)]
 
-EST = {"cy": 1.04, "pe": 0.55, "lat": 110.0, "fix": 30.0, "ga": 1.56, "far": 7.5, "near": 11.0, "first": 2000.0, "win": 150.0}
+EST = {"cy": 1.0, "pe": 0.63, "lat": 80.0, "fix": 15.0, "ga": 1.45, "far": 12.0, "near": 18.0, "port": 100.0, "loc": 500.0,
+       "first": 1300.0, "eng": 60.0, "call": 550.0, "tr": 80.0, "up": 1000.0, "wake": 400.0, "dma": 1250.0, "win": 30.0, "off": 500.0}
 CSEM = {"v": "cv", "a": "ca", "p": "cp", "g": "cg"}
 
 
 def starts(ws):
     out, x = [], 0
     for w in ws:
-        out.append((x, w))
+        out.append((x, x + w))
         x += w
     return out
 
@@ -71,292 +66,462 @@ def bits(m):
     return bin(m).count("1")
 
 
-def build(r, g, T, topo, arr):
-    ops = []
-    lab = [""]
-    core = T.cores[r]
+def build(r, cores, topo, ops, par):
+    core = cores[r]
     qs = list(range(r + 1, NR))
     nq = len(qs)
-    own = PAD + r * V
-    W = [lambda: T.W0, lambda: T.W1]
-    CY, PE, FIX, GA = EST["cy"], EST["pe"], EST["fix"], EST["ga"]
+    own = r * TW + GAP
+    W = ["W0", "W1"]
+    share = [{} for _ in range(NR)]
+    H = [0] * NR
+    for h in range(NR):
+        for x in par["PT"][h][1]:
+            if x[0] < 0:
+                share[x[2]].setdefault(h, []).append((H[x[2]], H[x[2]] - x[0]))
+                H[x[2]] -= x[0]
+    ups = [h for h in range(r + 1, NR) if any(h in share[o] for o in range(r + 1))]
+    naux = par["NAUX"]
+    tails = {}
 
-    def op(eng, dur, deps, fn, ext=(), kind="c", sem=None, tail=0.0, lat=0.0, send=None):
-        o = {"e": eng, "d": dur, "deps": [x for x in deps if x is not None], "fn": fn, "ext": list(ext), "k": kind,
-             "sem": sem, "tail": tail, "lat": lat, "send": send, "i": len(ops), "up": UP[r].get(lab[0] + eng, 0.0)}
+    def op(eng, cost, deps, fn, ext=(), kind="c", sem=None, send=None, lab="", line=None):
+        o = {"r": r, "e": eng, "c": cost, "deps": [x for x in deps if x is not None], "fn": fn, "ext": list(ext), "k": kind,
+             "sem": sem, "send": send, "i": len(ops), "lab": lab, "after": [tails[line]] if line in tails else [],
+             "up": par["UP"][r].get(lab + eng, 0.0)}
+        if line:
+            tails[line] = o
         ops.append(o)
         return o
 
-    def vc(n):
-        return max(64.0, n) * CY + FIX
-
     def V1(n, deps, fn, **kw):
-        return op("v", vc(n), deps, lambda: [fn()], **kw)
+        return op("v", ("v", n), deps, lambda g, T: [fn(g.vector, T)], **kw)
 
-    def A1(n, deps, fn, **kw):
-        return op("a", vc(n) + 20 + kw.pop("extra", 0), deps, lambda: [fn()], **kw)
+    def A1(n, deps, fn, table=None, **kw):
+        return op("a", ("a", n, table), deps, lambda g, T: [fn(g.scalar, T)], **kw)
 
     def G1(n, deps, fn):
-        return op("g", 170 + 2 * n * CY, deps, lambda: [fn()])
+        return op("g", ("g", n), deps, lambda g, T: [fn(g, T)])
+
+    def P1(n, deps, fn, **kw):
+        return op("p", ("p", n), deps, lambda g, T: fn(g.tensor, T), **kw)
 
     def over(lst, lo, hi):
         return [o for (a, b, o) in lst if a < hi and lo < b]
 
-    lds = []
-    tl = 1900.0
-    for j, (x0, w) in enumerate(starts(LC)):
-        tl += 128 * w * 4 / 220.0
-        q = "s" if j % 2 == 0 else "a"
-        lds.append(op(q, 60, [], lambda x0=x0, w=w, q=q: [(g.sync if q == "s" else g.scalar).dma_start(T.E[:, x0:x0 + w], T.ends[:, x0:x0 + w])],
-                      kind="d", sem="ld%d" % j, lat=tl, tail=1e6 - 1000 * j))
-    ldr = op("s", 60, [], lambda: [g.sync.dma_start(T.rt[:], T.rights[:])], kind="d", sem="lr", lat=tl, tail=9e5)
+    def mms(pu, n, terms):
+        return lambda t, T: [t.matmul(T[pu][:, 0:n], T[a][:, a0:a0 + 128], T[b][:, b0:b1:s], j == 0, j == len(terms) - 1) for j, (a, a0, b, b0, b1, s) in enumerate(terms)]
 
-    gA = G1(128, [], lambda: g.iota(T.Ai[:], [[-16, 8], [-1, 4], [-200, 4]], 0, 1, allow_small_or_imprecise_dtypes=True))
-    gD = G1(128, [], lambda: g.iota(T.Di[:], [[1, 128]], 0, -1, allow_small_or_imprecise_dtypes=True))
-    g4 = G1(4, [], lambda: g.iota(T.a4[:], [[0, 4]], 0, 1))
-    cS = [V1(128, [gA], lambda i=i: g.vector.tensor_scalar(T.S[:, 128 * i:128 * i + 128], T.Ai[:], -200.0 * i, None, A.is_equal)) for i in range(4)]
-    cK = V1(128, [gD], lambda: g.vector.tensor_scalar(T.Ik[:], T.Di[:], 0.0, K, A.is_equal, A.mult))
-    cM = cP = cO = cNB = cNT = None
+    lds = []
+    for j, (x0, x1) in enumerate(starts(par["LC"])):
+        q = "s" if j % 2 == 0 else "a"
+        lds.append(op(q, ("d", 512 * (x1 - x0)), [], lambda g, T, x0=x0, x1=x1, q=q: [(g.sync if q == "s" else g.scalar).dma_start(T.E[:, x0:x1], T.ends[:, x0:x1])],
+                      kind="d", sem="ld%d" % j, lab="ld", line="ld"))
+    ldr = op("s", ("d", 2048), [], lambda g, T: [g.sync.dma_start(T.rt[:], T.rights[:])], kind="d", sem="lr", lab="ld", line="ld")
+
+    g4 = G1(4, [], lambda g, T: g.iota(T.a4[:], [[0, 4]], 0, 1))
+    gD = G1(128, [], lambda g, T: g.iota(T.Di[:], [[1, 128]], 0, -1, allow_small_or_imprecise_dtypes=True))
+    c12 = V1(4, [g4], lambda v, T: v.tensor_scalar(T.a12[:], T.a4[:], 12, None, A.bitwise_and))
+    cro = V1(4, [c12], lambda v, T: v.tensor_scalar(T.row[:], T.a12[:], 0.0, None, A.is_equal))
+    cS, cS4 = [[V1(n, [gD, cro], lambda v, T, i=i, b=b: v.tensor_scalar(T[b][:, 128 * i:128 * i + 128], T.Di[:], 4.0 * i, T.row[:, 0:1], A.is_equal, A.mult))
+                for i in range(4 if on else 0)] for (b, n, on) in (("S", 64, True), ("S4", 128, par["RAW"][r]))]
+    cK = V1(128, [gD], lambda v, T: v.tensor_scalar(T.Ik[:], T.Di[:], 0.0, K, A.is_equal, A.mult))
+    cnt = []
     if nq:
-        cM = V1(64, [gD], lambda: g.vector.tensor_scalar(T.Im[:], T.Di[:], 0.0, -BIG, A.is_equal, A.mult))
-        cP = V1(64, [gD], lambda: g.vector.tensor_scalar(T.Ip[:], T.Di[:], 0.0, BIG, A.is_equal, A.mult))
-        cO = V1(OW, [], lambda: g.vector.memset(T.Ob[:], 0.0))
-        c1 = V1(64, [], lambda: g.vector.memset(T.n1[:], -1.0))
-        c2 = G1(128, [c1], lambda: g.affine_select(T.n2[:], T.n1[:], [[-4, 32], [0, 4]], A.is_ge, 0.0, 0, 1))
-        cNT = G1(128, [c2], lambda: g.affine_select(T.NT[:], T.n2[:], [[1, 128]], A.is_gt, 0.0, 0, -1))
-        cNB = G1(128, [c2], lambda: g.affine_select(T.NB[:], T.n2[:], [[4, 32], [0, 4]], A.is_ge, 0.0, 3, -1))
-    c4 = V1(4, [g4], lambda: g.vector.tensor_scalar(T.a4m[:], T.a4[:], 15, None, A.bitwise_and))
-    cf = V1(8, [c4, ldr], lambda: g.vector.tensor_tensor(T.rf[:], T.rt[:], T.a4m[:], A.subtract))
-    cQ = [V1(64, [cf, gD], lambda b=b: g.vector.tensor_scalar(T.Q[:, 128 * b:128 * b + 128], T.Di[:], T.rf[:, b:b + 1], None, A.is_equal)) for b in range(4)]
-    cT = V1(256, cQ, lambda: g.vector.transpose(T.P[:], T.Q[:]))
-    cz = V1(16, [], lambda: g.vector.memset(T.z0[:], 0.0), tail=1e5)
-    zero = [[], []]
-    for rd in range(2):
-        for col in (r * V, PAD + L):
-            zero[rd].append(A1(16, [cz], lambda rd=rd, col=col: g.scalar.activation(W[rd]()[:, col:col + PAD], T.z0[:], F.Exp, bias=-C * B, scale=C),
-                               extra=1300 if (rd == 0 and col == r * V) else 0, tail=1e5 if (rd == 0 and col == r * V) else 5e4))
+        gA = G1(128, [], lambda g, T: g.iota(T.A2[:], [[-16, 8], [0, 4], [-1, 4]], 0, 1, allow_small_or_imprecise_dtypes=True))
+        cf2 = V1(4, [c12], lambda v, T: v.tensor_copy(T.f12[:], T.a12[:]))
+        cNB = V1(64, [gA, cf2], lambda v, T: v.tensor_scalar(T.NB[:], T.A2[:], T.f12[:, 0:1], None, A.is_equal))
+        cNN = V1(64, [gA, cf2], lambda v, T: v.tensor_scalar(T.NN[:], T.A2[:], T.f12[:, 0:1], -1.0, A.is_equal, A.mult))
+        cNU = G1(128, [cNB], lambda g, T: g.affine_select(T.NU[:], T.NB[:], [[-1, 128]], A.is_gt, 0.0, 0, 1))
+        cM = V1(64, [gD], lambda v, T: v.tensor_scalar(T.Im[:], T.Di[:], 0.0, -BIG, A.is_equal, A.mult))
+        cG = V1(64, [gD], lambda v, T: v.tensor_scalar(T.Ig[:], T.Di[:], 0.0, float(GAP), A.is_equal, A.mult))
+        cTop = V1(Q4 / 2, [], lambda v, T: v.memset(T.top[:], TOP))
+        cND = V1(256, [cNU, cM], lambda v, T: v.tensor_tensor(T.ND[:], T.NU[:], T.Im[:], A.add))
+        cnt = [cNN, cND, cG]
+    c15 = V1(4, [g4], lambda v, T: v.tensor_scalar(T.a15[:], T.a4[:], 15, None, A.bitwise_and))
+    cf = V1(8, [c15, ldr], lambda v, T: v.tensor_tensor(T.rf[:], T.rt[:], T.a15[:], A.subtract))
+    cQ = [V1(64, [cf, gD], lambda v, T, b=b: v.tensor_scalar(T.Q[:, 128 * b:128 * b + 128], T.Di[:], T.rf[:, b:b + 1], None, A.is_equal)) for b in range(4)]
+    cT = V1(256, cQ, lambda v, T: v.transpose(T.P[:], T.Q[:]))
+    cR = V1(256, [], lambda v, T: v.memset(T.rt2[0:32, :], ROOT)) if "a" in par["ED"][r] else None
+    cz = V1(16, [], lambda v, T: v.memset(T.z0[:], 0.0))
+    gap = [A1(16, [cz], lambda a, T: a.activation(T.W0[:, own - GAP:own], T.z0[:], F.Exp, bias=-C * B, scale=C), table="exp", line="ld"),
+           V1(16, [], lambda v, T: v.memset(T.W1[:, own - GAP:own], 0.0))]
+    end = [V1(16, [], lambda v, T, rd=rd: v.memset(T[W[rd]][:, NR * TW:WW], 0.0)) for rd in range(2)]
 
     wr = [[], []]
-    for j, (x0, w) in enumerate(starts(LC)):
-        cv = V1(w, [lds[j]], lambda x0=x0, w=w: g.vector.tensor_copy(T.X[:, x0:x0 + w], T.E[:, x0:x0 + w]))
-        wr[0].append((x0, x0 + w, A1(w, [cv], lambda x0=x0, w=w: g.scalar.activation(T.W0[:, own + x0:own + x0 + w], T.X[:, x0:x0 + w], F.Exp, bias=-C * B, scale=C))))
-    allexp = [o for (_, _, o) in wr[0]] + zero[0] + zero[1]
+    cvs = []
+    for j, (x0, x1) in enumerate(starts(par["LC"])):
+        cv = V1(x1 - x0, [lds[j]], lambda v, T, x0=x0, x1=x1: v.tensor_copy(T.X[:, x0:x1], T.E[:, x0:x1]), lab="cv")
+        cvs.append((x0, x1, cv))
+        wr[0].append((x0, x1, A1(x1 - x0, [cv, gap[0]], lambda a, T, x0=x0, x1=x1: a.activation(T.W0[:, own + x0:own + x1], T.X[:, x0:x1], F.Exp, bias=-C * B, scale=C), table="exp", lab="ex")))
+    allexp = [o for (_, _, o) in wr[0]]
 
-    st = {"R": None, "U": [None, None], "M": [None] * NMAIN, "nb": 0, "nu": 0, "ln": 0}
+    st = {"bank": [None] * naux + [[]] * (8 - naux), "nm": 0, "nu": 0, "ns": 0}
+
+    def aux():
+        st["nu"] += 1
+        return (st["nu"] - 1) % naux
+
+    def lnop(n, deps, fn, lab):
+        return A1(n, deps + allexp, fn, table="ln", lab=lab)
 
     def index(rd):
-        fins, scans = [], []
-        lab[0] = "i%d" % rd
-        for c, (x0, w) in enumerate(starts(CH[r][rd])):
-            n, k0 = w // 4, x0 // 4
-            ns = n + 2
-            lc = 448 * rd + k0
-            rel = op("p", 4 * max(64, n) * PE + FIX, over(wr[rd], x0, x0 + w) + cS + [st["R"]],
-                     lambda rd=rd, x0=x0, n=n: [g.tensor.matmul(T.pR[:, 0:n], T.S[:, 128 * i:128 * i + 128], W[rd]()[:, own + x0 + n * i:own + x0 + n * i + n], i == 0, i == 3) for i in range(4)])
-            ln = A1(n, [rel] + allexp, lambda lc=lc, n=n: g.scalar.activation(T.Ln[:, lc:lc + n], T.pR[:, 0:n], F.Ln), extra=1500 if st["ln"] == 0 else 0)
-            st["ln"] = 1
-            st["R"] = ln
-            u = st["nu"] % 2
-            st["nu"] += 1
-            pu = "pU%d" % u
-            terms, deps = [], [ln, cK, st["U"][u]]
-            if nq:
-                ob = OW * rd + k0 + 2 * c
-                mb = nq * ob
-                sc0, bi0 = K / V, (B + 0.5) / V - 0.5 + OB
-                if EO[r][rd] == "v":
-                    o1 = V1(n, [ln, cO], lambda lc=lc, n=n, ob=ob: g.vector.tensor_scalar(T.Ob[:, ob + 2:ob + 2 + n], T.Ln[:, lc:lc + n], sc0, bi0, A.mult, A.add))
-                else:
-                    o1 = A1(n, [ln, cO], lambda lc=lc, n=n, ob=ob: g.scalar.activation(T.Ob[:, ob + 2:ob + 2 + n], T.Ln[:, lc:lc + n], F.Identity, bias=bi0, scale=sc0))
-                ms = [V1(ns / 2, [o1], lambda ob=ob, ns=ns, a=mb + j * ns, q=q: g.vector.tensor_scalar(T.mb[:, a:a + ns], T.Ob[:, ob:ob + ns], OB + q, None, A.is_equal)) for j, q in enumerate(qs)]
-                sc = [V1(ns / 2, [ms[j]], lambda a=mb + j * ns, ns=ns: g.vector.tensor_tensor_scan(T.cb[:, a:a + ns], T.mb[:, a:a + ns], T.mb[:, a:a + ns], 0.0, A.add, A.max)) for j in range(nq)]
-                scans.append((mb, ns, sc))
-                ca = op("p", 64 * len(scans) * PE + FIX, [x for (_, _, s) in scans for x in s] + [cNT, cNB, st["U"][u]],
-                        lambda sl=[(a, b) for (a, b, _) in scans], pu=pu: [g.tensor.matmul(T[pu][:, 0:nq], (T.NT if j == len(sl) - 1 else T.NB)[:], T.cb[:, a + b - 1:a + nq * b:b], j == 0, j == len(sl) - 1) for j, (a, b) in enumerate(sl)])
-                sat = [V1(ns / 2, [ca], lambda a=mb + j * ns, ns=ns, j=j, pu=pu: g.vector.tensor_scalar(T.sb[:, a:a + ns], T.cb[:, a:a + ns], -float(CAP), T[pu][:, j:j + 1], A.add, A.max)) for j in range(nq)]
-                deps += sat + [cM, cP]
-                for j in range(nq):
-                    terms += [("Im", "sb", mb + j * ns + 2), ("Ip", "sb", mb + j * ns + 1)]
+        fins, prev = [], None
+        lab = "i%d" % rd
+        eo, ef, ez = par["EI"][r][rd]
+        for (x0, x1) in starts(par["IC"][r][rd]):
+            n, k0 = (x1 - x0) // 4, x0 // 4
+            lab = ("j%d" if x1 == V else "i%d") % rd
+            lc = Q4 * rd + k0
+            u = aux()
+            pu = "ps%d" % u
+            raw = rd == 0 and len(fins) < par["RAW"][r]
+            if raw:
+                lay = [("S4", 128 * i, "X", x0 + i, x1, 4) for i in range(4)]
+                t = rel = P1(16 * max(64, n), over(cvs, x0, x1) + cS4 + [st["bank"][u]], mms(pu, n, lay), lab=lab)
+                s0, b0, terms, cost = 1.0, 0.0, [], 0
+                if nq:
+                    raw = False
+                    t = A1(n, [rel], lambda a, T, lc=lc, n=n, pu=pu: a.activation(T.Ln[:, lc:lc + n], T[pu][:, 0:n], F.Identity, bias=-C * B, scale=C), lab=lab)
+                    s0, b0 = K, B
+                    terms, cost = [("Ik", 0, "Ln", lc, lc + n, 1)], 4 * max(64, n)
+            else:
+                lay = [("S", 128 * i, W[rd], own + x0 + i, own + x1, 4) for i in range(4)]
+                rel = P1(4 * max(64, n), over(wr[rd], x0, x1) + cS + [st["bank"][u]], mms(pu, n, lay), lab=lab)
+                t = lnop(n, [rel], lambda a, T, lc=lc, n=n, pu=pu: a.activation(T.Ln[:, lc:lc + n], T[pu][:, 0:n], F.Ln), lab)
+                s0, b0 = K, B
+                terms, cost = [("Ik", 0, "Ln", lc, lc + n, 1)], 4 * max(64, n)
+            deps = [t, cK]
             if r == 0:
-                if EZ[rd] == "v":
-                    deps.append(V1(n, [ln], lambda lc=lc, n=n: g.vector.tensor_scalar(T.zb[:, lc:lc + n], T.Ln[:, lc:lc + n], C * (0.5 - B), None, A.is_lt)))
+                if ez == "v":
+                    z = V1(n, [t], lambda v, T, lc=lc, n=n: v.tensor_scalar(T.zb[:, lc:lc + n], T.Ln[:, lc:lc + n], C * (0.5 - B), None, A.is_lt), lab=lab)
                 else:
-                    deps.append(A1(n, [ln], lambda lc=lc, n=n: g.scalar.activation(T.zb[:, lc:lc + n], T.Ln[:, lc:lc + n], F.Relu, bias=800.0 * C * (0.5 - B), scale=-800.0)))
-                terms.append(("Im", "zb", lc))
-            terms.append(("Ik", "Ln", lc))
-            um = op("p", (len(terms) + 3) * max(64, n) * PE + FIX, deps,
-                    lambda terms=terms, n=n, pu=pu: [g.tensor.matmul(T[pu][:, 8:8 + n], T[a][:], T[b][:, x:x + n], j == 0, j == len(terms) - 1) for j, (a, b, x) in enumerate(terms)])
-            fin = V1(n, [um], lambda lc=lc, n=n, pu=pu: g.vector.tensor_scalar(T.off[:, lc:lc + n], T[pu][:, 8:8 + n], MAGIC + B + PAD - r * V, MAGIC, A.add, A.subtract))
-            st["U"][u] = fin
-            fins.append(fin)
+                    z = A1(n, [t], lambda a, T, lc=lc, n=n: a.activation(T.zb[:, lc:lc + n], T.Ln[:, lc:lc + n], F.Relu, bias=8.0 * (0.5 - B), scale=-8.0 * K), lab=lab)
+                terms.append(("Im", 0, "zb", lc, lc + n, 1))
+                cost += max(64, n)
+                deps.append(z)
+            if nq:
+                mb = nq * lc
+                sc0, bi0 = K / V, (B + 0.5) / V - 0.5 + OB
+                if eo == "v":
+                    o1 = V1(n, [t], lambda v, T, lc=lc, n=n: v.tensor_scalar(T.Ob[:, lc:lc + n], T.Ln[:, lc:lc + n], sc0, bi0, A.mult, A.add), lab=lab)
+                else:
+                    o1 = A1(n, [t], lambda a, T, lc=lc, n=n: a.activation(T.Ob[:, lc:lc + n], T.Ln[:, lc:lc + n], F.Identity, bias=bi0, scale=sc0), lab=lab)
+                ms = [V1(n / 2, [o1], lambda v, T, lc=lc, n=n, a=mb + j * n, q=q: v.tensor_scalar(T.mb[:, a:a + n], T.Ob[:, lc:lc + n], OB + q, None, A.is_equal), lab=lab) for j, q in enumerate(qs)]
+                sc = []
+                for j in range(nq):
+                    pa = None if prev is None else prev[0] + (j + 1) * prev[1] - 1
+                    sc.append(V1(n / 2, [ms[j], cTop] + ([] if prev is None else [prev[2][j]]),
+                                 lambda v, T, a=mb + j * n, n=n, pa=pa: v.tensor_tensor_scan(T.cb[:, a:a + n], T.mb[:, a:a + n], T.top[:, 0:n], 0.0 if pa is None else T.cb[:, pa:pa + 1], A.add, A.min), lab=lab))
+                prev = (mb, n, sc)
+                m = nq * n
+                ca = P1(2 * max(64, m), sc + cnt, mms(pu, m, [("NN", 0, "cb", mb, mb + m, 1), ("ND", 0, "mb", mb, mb + m, 1)]), lab=lab)
+                if ef == "v":
+                    fl = V1(m, [ca], lambda v, T, mb=mb, m=m, pu=pu: v.tensor_scalar(T.fb[:, mb:mb + m], T[pu][:, 0:m], -BIG - CAP - 0.5, None, A.is_lt), lab=lab)
+                else:
+                    fl = A1(m, [ca], lambda a, T, mb=mb, m=m, pu=pu: a.activation(T.fb[:, mb:mb + m], T[pu][:, 0:m], F.Relu, bias=-BIG - CAP, scale=-1.0), lab=lab)
+                deps.append(fl)
+                terms += [("Ig", 0, "Ob", lc, lc + n, 1)] + [("Im", 0, "fb", mb + j * n, mb + j * n + n, 1) for j in range(nq)]
+                cost += (nq + 1) * max(64, n)
+                shift = b0 + GAP * (1 - OB) - r * TW
+            else:
+                shift = b0 + GAP * NR - r * TW
+            um = rel if raw else P1(cost, deps, mms(pu, n, terms), lab=lab)
+            fin = V1(n, [um], lambda v, T, lc=lc, n=n, pu=pu, shift=shift: v.tensor_scalar(T.off[:, lc:lc + n], T[pu][:, 0:n], MAGIC + shift, MAGIC, A.add, A.subtract), lab=lab)
+            st["bank"][u] = fin
+            fins.append((x0, x1, fin))
         return fins
 
     def arrivals(rd):
-        if r == 1:
-            names = ["f%d_%d_%d" % (rd, s, p) for s in (2, 3) for p in range(len(PC[rd]))]
-        elif r == 3:
-            names = []
-        else:
-            names = ["a%d" % rd]
-        return [(s, arr[(r, s)][1], arr[(r, s)][0]) for s in names]
+        hub = par["HUB"][rd]
+        fs = ["f%d_%d_%d" % (rd, s, p) for s in (2, 3) if hub[s - 2] == r for p in range(len(par["PC"][rd][s - 2]))]
+        return fs + ([] if r == 3 or (r == 1 and 0 not in hub) else ["a%d" % rd])
+
+    def tr(dst, sb, s0, db, d0, w, size, mask, sem):
+        return {"dst": dst, "sb": sb, "s0": s0, "db": db, "d0": d0, "w": w, "by": 128 * w * size, "mask": mask, "sem": sem}
+
+    def snd(lst, deps, ext=(), line=None, lab="snd"):
+        def fn(g, T):
+            out = []
+            for x in lst:
+                rid, pid = topo.addr(cores[x["dst"]], core)
+                out.append(RemoteDMATransfer(dst_ids=[DstId(rid=rid, pnc=pid)], dma_engine_mask=x["mask"], remote_sem=T.sem[x["sem"]],
+                                             src=T[x["sb"]][:, x["s0"]:x["s0"] + x["w"]], dst=T[x["db"]][:, x["d0"]:x["d0"] + x["w"]]))
+            return [g.remote_dma_fused(out, local_sem=T.sem.sent)]
+        return op("g", ("r",), deps, fn, ext=ext, kind="r", send=lst, lab=lab, line=line)
+
+    def msk(dst):
+        return topo.mask(core, cores[dst])
+
+    def half(m):
+        en = [e for e in range(m.bit_length()) if m >> e & 1]
+        lo = sum(1 << e for e in en[:len(en) // 2])
+        return lo, m & ~lo
+
+    def upmask(hs):
+        m = msk(hs[0]) & ~(msk(1) if r == 2 else 0) if hs else 0
+        return [m] if len(hs) == 1 else half(m)
+
+    def store(deps, ext, src, x0, x1):
+        st["ns"] += 1
+        op("s", ("d", 512 * (x1 - x0)), deps, lambda g, T: [g.sync.dma_start(T.y[:, x0:x1], T[src][:, x0:x1])], ext=ext, kind="d", sem="st%d" % (st["ns"] - 1), lab="st")
 
     def main(rd, fins):
         res = []
-        tbl = [o for (_, _, o) in wr[rd]] + zero[rd]
-        for c, (x0, w) in enumerate(starts(CH[r][rd])):
-            n, lc = w // 4, 448 * rd + x0 // 4
-            kv = VS[r][rd][c]
+        tbl = [o for (_, _, o) in wr[rd]] + [gap[rd], end[rd]]
+        nx = {o: share[o][r][0][0] for o in range(r) if r in share[o]}
+        nx[r] = H[r] if rd else 0
+        for pn, part in enumerate(par["PT"][r][rd]):
+            w, wv = part[:2]
+            ed = par["ED"][r][pn]
+            mine = w > 0
+            w = abs(w)
+            o = r if mine else part[2]
+            x0 = nx[o]
+            x1 = nx[o] = x0 + w
+            Gb, Pb, Fb, Xb, ob = [n + ("" if mine else "h%d" % (r - o)) for n in ("G", "P", "F", "X", "off")]
+            oc = Q4 * rd if mine else 0
+            ext = arrivals(rd) + ([] if mine else ["h%d" % o] + ["t%d" % q for q in range(o, r)])
+            deps = tbl + (over(fins, x0, x1) if mine else [])
             gs = []
-            lab[0] = "g%d" % rd
 
-            def win(rd, a, b):
-                return W[rd]()[:, r * V:WW].indirect(T.off[:, a:b])
-            if kv:
-                gs.append(V1(16 * kv * GA, tbl + [fins[c]], lambda rd=rd, lc=lc, kv=kv, x0=x0: g.vector.tensor_copy(T.G[:, 4 * x0:4 * x0 + 16 * kv], win(rd, lc, lc + kv)), ext=arrivals(rd)))
-            if kv < n:
-                gs.append(A1(16 * (n - kv) * GA, tbl + [fins[c]], lambda rd=rd, lc=lc, kv=kv, x0=x0, n=n: g.scalar.activation(T.G[:, 4 * x0 + 16 * kv:4 * x0 + 16 * n], win(rd, lc + kv, lc + n), F.Copy), ext=arrivals(rd)))
-            lab[0] = "m%d" % rd
-            parts = [(0, 4)] if w <= 512 else [(0, 2), (2, 4)]
-            prev = [None] * len(parts)
+            def win(T, a, b, o=o, ob=ob, oc=oc):
+                return T[W[rd]][:, o * TW:WW].indirect(T[ob][:, oc + a // 4:oc + b // 4])
+            if wv:
+                gs.append(op("v", ("gv", 4 * wv), deps, lambda g, T, a=x0, b=x0 + wv, win=win, Gb=Gb: [g.vector.tensor_copy(T[Gb][:, 4 * a:4 * b], win(T, a, b))], ext=ext, lab="g%d" % rd, line=par["LN"][0]))
+            if wv < w:
+                gs.append(op("a", ("ga", 4 * (w - wv)), deps, lambda g, T, a=x0 + wv, b=x1, win=win, Gb=Gb: [g.scalar.activation(T[Gb][:, 4 * a:4 * b], win(T, a, b), F.Copy)], ext=ext, lab="g%d" % rd, line=par["LN"][1]))
+            cut = [(x0, x1)] if w < par["SPLIT"] else [(x0, x0 + w // 2), (x0 + w // 2, x1)]
+            prev = [None] * len(cut)
+            c0 = o * TW + GAP
             for b in range(4):
-                for h, (i0, i1) in enumerate(parts):
-                    bk = st["nb"] % NMAIN
-                    st["nb"] += 1
-                    pm = "pm%d" % bk
-                    mm = op("p", (i1 - i0) * max(64, n) * PE + FIX, gs + [cT, st["M"][bk]],
-                            lambda pm=pm, b=b, n=n, x0=x0, i0=i0, i1=i1: [g.tensor.matmul(T[pm][:, n * (i - i0):n * (i - i0) + n], T.P[:, 128 * b:128 * b + 128], T.G[:, 4 * x0 + 4 * b + i:4 * x0 + 16 * n:16], True, True) for i in range(i0, i1)])
-
-                    def mx(pm=pm, b=b, xa=x0 + n * i0, xb=x0 + n * i1, rd=rd):
-                        dst = T.W1[:, own + xa:own + xb] if rd == 0 else T.Fo[:, xa:xb]
-                        src = W[rd]()[:, own + xa:own + xb] if b == 0 else dst
-                        return g.vector.tensor_tensor(dst, T[pm][:, 0:xb - xa], src, A.max)
-                    prev[h] = V1(n * (i1 - i0), [mm, prev[h]], mx)
-                    st["M"][bk] = prev[h]
-            for h, (i0, i1) in enumerate(parts):
-                res.append((x0 + n * i0, x0 + n * i1, prev[h]))
+                bk = naux + st["nm"] % (8 - naux)
+                st["nm"] += 1
+                pm = "ps%d" % bk
+                mm = P1(max(64, w), gs + [cT if mine else None] + st["bank"][bk], mms(pm, w, [(Pb, 128 * b, Gb, 4 * x0 + b, 4 * x1, 4)]), lab="m%d" % rd)
+                for h, (xa, xb) in enumerate(cut):
+                    def mx(v, T, pm=pm, b=b, x0=x0, xa=xa, xb=xb, c0=c0, Fb=Fb):
+                        dst = T.W1[:, c0 + xa:c0 + xb] if rd == 0 else T[Fb][:, xa:xb]
+                        src = T[W[rd]][:, c0 + xa:c0 + xb] if b == 0 else dst
+                        return v.tensor_tensor(dst, T[pm][:, xa - x0:xb - x0], src, A.max)
+                    prev[h] = V1(xb - xa, [mm, prev[h]], mx, lab="m%d" % rd, line=par["LN"][2])
+                st["bank"][bk] = list(prev)
+            res += [(xa, xb, prev[h]) for h, (xa, xb) in enumerate(cut)]
+            if rd:
+                ln = lnop(w, prev, lambda a, T, x0=x0, x1=x1, Xb=Xb, Fb=Fb: a.activation(T[Xb][:, x0:x1], T[Fb][:, x0:x1], F.Ln), "d")
+                u = aux() if ed in "va" else None
+                pu = "ps%s" % u
+                if u is None:
+                    if ed in "xy":
+                        d1 = A1(w, [ln], lambda a, T, x0=x0, x1=x1, Xb=Xb: a.activation(T[Xb][:, x0:x1], T[Xb][:, x0:x1], F.Identity, bias=MAGIC + B, scale=K), lab="d")
+                    else:
+                        d1 = V1(w, [ln], lambda v, T, x0=x0, x1=x1, Xb=Xb: v.tensor_scalar(T[Xb][:, x0:x1], T[Xb][:, x0:x1], K, MAGIC + B, A.mult, A.add), lab="d")
+                    if ed == "y":
+                        d2 = A1(w, [d1], lambda a, T, x0=x0, x1=x1, Xb=Xb: a.activation(T[Xb][:, x0:x1], T[Xb][:, x0:x1], F.Identity, bias=-MAGIC), lab="d")
+                    else:
+                        d2 = V1(w, [d1], lambda v, T, x0=x0, x1=x1, Xb=Xb: v.tensor_scalar(T[Xb][:, x0:x1], T[Xb][:, x0:x1], MAGIC, None, A.subtract), lab="d")
+                elif ed == "v":
+                    d1 = P1(4 * max(64, w), [ln, cK, st["bank"][u]], mms(pu, w, [("Ik", 0, Xb, x0, x1, 1)]), lab="d")
+                    d2 = V1(w, [d1], lambda v, T, x0=x0, x1=x1, pu=pu, Xb=Xb: v.tensor_scalar(T[Xb][:, x0:x1], T[pu][:, 0:x1 - x0], MAGIC + B, MAGIC, A.add, A.subtract), lab="d")
+                else:
+                    d1 = P1(5 * max(64, w), [ln, cK, cR, st["bank"][u]], lambda t, T, x0=x0, x1=x1, pu=pu, Xb=Xb: [
+                        t.matmul(T[pu][:, 0:x1 - x0], T.Ik[:], T[Xb][:, x0:x1], True, False),
+                        t.matmul(T[pu][:, 0:x1 - x0], T.rt2[0:1, 0:128], T.rt2[0:1, 0:x1 - x0], False, True)], lab="d")
+                    d2 = A1(w, [d1], lambda a, T, x0=x0, x1=x1, pu=pu, Xb=Xb: a.activation(T[Xb][:, x0:x1], T[pu][:, 0:x1 - x0], F.Identity, bias=B - ROOT * ROOT), lab="d")
+                if u is not None:
+                    st["bank"][u] = d2
+                if mine:
+                    store([d2], [], "X", x0, x1)
+                else:
+                    back = [x for h in sorted(share[o]) for x in share[o][h]].index((x0, x1))
+                    snd([tr(o, Xb, x0, "Yl", x0, w, 4, msk(o), "y%d" % back)], [d2])
         return res
 
-    def sends(rd):
-        lab[0] = "s"
+    def sends(rd, fins):
+        def pieces(ws):
+            return [(a - (GAP if a == 0 else 0), b) for (a, b) in starts(ws)]
 
-        def tr(dst, src, a, b, mask, sem):
-            rid, pid = topo.addr(T.cores[dst], core)
-            ap = W[rd]()[:, PAD + src * V + a:PAD + src * V + b]
-            return RemoteDMATransfer(dst_ids=[DstId(rid=rid, pnc=pid)], dma_engine_mask=mask, remote_sem=T.sem[sem], src=ap, dst=ap)
+        def tb(dst, src, a, b, mask, sem):
+            c = src * TW + GAP + a
+            return tr(dst, W[rd], c, W[rd], c, b - a, 2, mask, sem)
+        hub = par["HUB"][rd]
+        pcs = {s: pieces(par["PC"][rd][s - 2]) for s in (2, 3)}
+        on = {s: pcs[s][:max(0, len(pcs[s]) - par["DUP"][rd][s - 2])] for s in (2, 3)}
 
-        def snd(lst, deps, ext, tail):
-            op("g", 400, deps, lambda lst=lst: [g.remote_dma_fused([tr(*x) for x in lst], local_sem=T.sem.sent)], ext=ext, kind="r", send=lst, tail=tail)
-        rest = 14000.0 * (2 - rd) + 4000
+        def own_piece(lst, a, b):
+            deps = over(wr[rd], a, b) + [gap[rd]]
+            if rd:
+                lst = lst + [tb(h, r, a, b, m, "t%d" % r) for h, m in zip(ups, upmask(ups))]
+            if rd and share[r] and b == V:
+                n, hs = b - a, sorted(share[r])
+                if par["FO"][r] and len(ups) == 1 and H[r] <= 4 * n <= V:
+                    lst[-1]["mask"], m = half(lst[-1]["mask"])
+                    return snd(lst + [tr(hs[0], "off", Q4, "offh%d" % (hs[0] - r), 0, n, 2, m, "h%d" % r)], deps + over(fins, 0, 4 * n), line="own")
+                snd([tr(h, "off", Q4, "offh%d" % (h - r), 0, H[r] // 4, 2, m, "h%d" % r) for h, m in zip(hs, upmask(hs))], over(fins, 0, H[r]))
+            if lst:
+                snd(lst, deps, line="own")
         if r >= 2:
-            far = topo.mask(core, T.cores[1])
-            en = topo.engines(core, T.cores[1])
-            lo = sum(1 << e for e in en[:len(en) // 2])
-            for p, (a, b) in enumerate(PC[rd]):
-                if p in DUP[rd]:
-                    lst = [(1, r, a, b, lo, "f%d_%d_%d" % (rd, r, p)), (0, r, a, b, far & ~lo, "a%d" % rd)]
+            far = msk(1)
+            for p, (a, b) in enumerate(pcs[r]):
+                if p >= len(on[r]):
+                    lst = [tb(hub[r - 2], r, a, b, half(far)[0], "f%d_%d_%d" % (rd, r, p)), tb(1 - hub[r - 2], r, a, b, half(far)[1], "a%d" % rd)]
                 else:
-                    lst = [(1, r, a, b, far, "f%d_%d_%d" % (rd, r, p))]
+                    lst = [tb(hub[r - 2], r, a, b, far, "f%d_%d_%d" % (rd, r, p))]
                 if r == 3:
-                    lst.append((2, r, a, b, topo.mask(core, T.cores[2]) & ~far, "a%d" % rd))
-                snd(lst, over(wr[rd], a, b), [], rest + 9000 - 2000 * p)
-        if r == 1:
-            full = topo.mask(core, T.cores[0])
-            en = topo.engines(core, T.cores[0])
-            lo = sum(1 << e for e in en[:len(en) // 2])
-            for p, (a, b) in enumerate(PO[rd]):
-                snd([(0, 1, a, b, full, "a%d" % rd)], over(wr[rd], a, b), [], rest + 3000 - 500 * p)
-            for p, (a, b) in enumerate(PC[rd]):
-                if p in DUP[rd]:
-                    continue
-                ext = [(s, arr[(r, s)][1], arr[(r, s)][0]) for s in ("f%d_2_%d" % (rd, p), "f%d_3_%d" % (rd, p))]
-                snd([(0, 2, a, b, lo, "a%d" % rd), (0, 3, a, b, full & ~lo, "a%d" % rd)], [], ext, rest + 3000 - 500 * p)
+                    lst.append(tb(2, r, a, b, msk(2) & ~far, "a%d" % rd))
+                own_piece(lst, a, b)
+        else:
+            for (a, b) in pieces(par["PO"][r][rd]):
+                own_piece([tb(0, 1, a, b, msk(0) & ~(msk(2) if rd and ups else 0), "a%d" % rd)] if r else [], a, b)
+        if r < 2:
+            lo, hi = half(msk(1 - r))
+            both = [x for x, y in zip(on[2], on[3]) if x == y and hub == [r, r]]
+            for (a, b) in both:
+                p = on[2].index((a, b))
+                snd([tb(1 - r, 2, a, b, lo, "a%d" % rd), tb(1 - r, 3, a, b, hi, "a%d" % rd)], [], ["f%d_2_%d" % (rd, p), "f%d_3_%d" % (rd, p)], line="on2")
+            for s in (2, 3):
+                for p, (a, b) in enumerate(on[s]):
+                    if hub[s - 2] == r and (a, b) not in both:
+                        snd([tb(1 - r, s, a, b, hi if rd and r else lo | hi, "a%d" % rd)], [], ["f%d_%d_%d" % (rd, s, p)], line="on%d" % s)
 
-    sends(0)
+    sends(0, None)
+    if H[r]:
+        snd([tr(h, "P", 0, "Ph%d" % (h - r), 0, 512, 2, m, "h%d" % r) for h, m in zip(sorted(share[r]), upmask(sorted(share[r])))], [cT])
     f0 = index(0)
     wr[1] = main(0, f0)
-    sends(1)
     f1 = index(1)
-    last = main(1, f1)
-    lab[0] = "d"
-    for c, (x0, x1, o) in enumerate(last):
-        w = x1 - x0
-        ln = A1(w, [o], lambda x0=x0, x1=x1: g.scalar.activation(T.X[:, x0:x1], T.Fo[:, x0:x1], F.Ln))
-        if DEC[r][c] == "p":
-            u = st["nu"] % 2
-            st["nu"] += 1
-            d1 = op("p", 4 * w * PE + FIX, [ln, st["U"][u]], lambda x0=x0, x1=x1, u=u: [g.tensor.matmul(T["pU%d" % u][:, 0:x1 - x0], T.Ik[:], T.X[:, x0:x1], True, True)])
-            d2 = V1(w, [d1], lambda x0=x0, x1=x1, u=u: g.vector.tensor_scalar(T.X[:, x0:x1], T["pU%d" % u][:, 0:x1 - x0], MAGIC + B, MAGIC, A.add, A.subtract))
-            st["U"][u] = d2
-        else:
-            if DEC[r][c] == "a":
-                d1 = A1(w, [ln], lambda x0=x0, x1=x1: g.scalar.activation(T.X[:, x0:x1], T.X[:, x0:x1], F.Identity, bias=MAGIC + B, scale=K))
-            else:
-                d1 = V1(w, [ln], lambda x0=x0, x1=x1: g.vector.tensor_scalar(T.X[:, x0:x1], T.X[:, x0:x1], K, MAGIC + B, A.mult, A.add))
-            d2 = V1(w, [d1], lambda x0=x0, x1=x1: g.vector.tensor_scalar(T.X[:, x0:x1], T.X[:, x0:x1], MAGIC, None, A.subtract))
-        op("s", 60, [d2], lambda x0=x0, x1=x1: [g.sync.dma_start(T.y[:, x0:x1], T.X[:, x0:x1])], kind="d", sem="st%d" % c, lat=1900 + 128 * w * 4 / 220.0)
-    return ops
+    sends(1, f1)
+    for j, (x0, x1) in enumerate([x for h in sorted(share[r]) for x in share[r][h]]):
+        store([], ["y%d" % j], "Yl", x0, x1)
+    main(1, f1)
 
 
-def order(ops):
-    LAT = EST["lat"]
-    users = [[] for _ in ops]
+def dur(o, M):
+    c = o["c"]
+    k = c[0]
+    if k == "v":
+        return max(64.0, c[1]) * M["cy"] + M["fix"]
+    if k == "a":
+        return max(64.0, c[1]) * M["cy"] + M["fix"] + 20
+    if k == "gv" or k == "ga":
+        return c[1] * M["ga"] * M["cy"] + (50 if k == "gv" else 65)
+    if k == "p":
+        return c[1] * M["pe"] + M["fix"]
+    if k == "g":
+        return 170 + 2 * c[1] * M["cy"]
+    return M["call"] + M["tr"] * len(o["send"]) if k == "r" else 60.0
+
+
+def run(o, t, S, M, cores, topo):
+    r = o["r"]
+    o["t"] = t
+    if o["c"][0] == "a" and o["c"][2] and S.get(("table", r)) != o["c"][2]:
+        S[("table", r)] = o["c"][2]
+        o["d"] += 1400.0
+    o["end"] = S[(r, o["e"])] = t + o["d"]
+    if o["k"] == "d":
+        t1 = max([o["end"] + M["dma"]] + [S.get((r, e), 0.0) for e in range(16)]) + o["c"][1] / M["loc"]
+        for e in range(16):
+            S[(r, e)] = t1
+        o["end"] = t1
+    if o["k"] == "r":
+        new = [e for x in o["send"] for e in range(16) if x["mask"] >> e & 1 and ("u", r, e) not in S]
+        t0 = o["end"] + M["up"] + M["eng"] * len(new) + (0.0 if ("u", r) in S else M["first"])
+        S[("u", r)] = 1
+        for x in o["send"]:
+            far = topo.host(cores[x["dst"]]) != topo.host(cores[r])
+            es = [e for e in range(16) if x["mask"] >> e & 1]
+            t1 = max([t0 + (M["off"] if far else 0.0)] + [S.get((r, e), 0.0) for e in es]) + x["by"] / ((M["far"] if far else M["near"]) * len(es))
+            if far:
+                S[("port", r)] = max(t0, S.get(("port", r), 0.0)) + x["by"] / M["port"]
+                t1 = max(t1, S[("port", r)])
+            for e in es:
+                S[(r, e)] = t1
+                S[("u", r, e)] = 1
+            key = ("land", x["dst"], x["sem"])
+            S[key] = max(S.get(key, 0.0), t1 + M["wake"])
+            o["land"] = t1 + M["wake"]
+
+
+def ready(o, S, M):
+    return max([0.0] + [d["t"] for d in o["after"]] + [d["end"] + M["lat"] for d in o["deps"]] + [S[("land", o["r"], s)] for s in o["ext"]])
+
+
+def plan(cores, topo, par=PAR, M=EST):
+    ops = []
+    for r in range(NR):
+        build(r, cores, topo, ops, par)
+    src, total = {}, {}
     for o in ops:
-        for d in o["deps"]:
-            users[d["i"]].append(o)
-    for o in reversed(ops):
-        o["pr"] = o["d"] + o["lat"] + max([o["tail"]] + [u["pr"] + LAT for u in users[o["i"]]])
+        o["d"] = dur(o, M)
+        for x in o["send"] or []:
+            src.setdefault((x["dst"], x["sem"]), []).append(o)
+            total[(x["dst"], x["sem"])] = total.get((x["dst"], x["sem"]), 0) + bits(x["mask"])
+    users = [[] for _ in ops]
+    left = []
+    for o in ops:
+        pre = {d["i"] for d in o["deps"] + o["after"]} | {d["i"] for s in o["ext"] for d in src[(o["r"], s)]}
+        left.append(len(pre))
+        for i in pre:
+            users[i].append(o)
+    n, chain = list(left), [o for o in ops if not left[o["i"]]]
+    for o in chain:
+        for u in users[o["i"]]:
+            n[u["i"]] -= 1
+            if not n[u["i"]]:
+                chain.append(u)
+    for o in reversed(chain):
+        lat = M["lat"]
+        if o["k"] == "d":
+            lat += M["dma"] + o["c"][1] / M["loc"]
+        if o["k"] == "r":
+            lat += M["up"] + M["wake"] + o["send"][0]["by"] / M["port"]
+        if o["lab"] in ("i0", "i1"):
+            lat += par["HOP"][o["r"]]
+        o["pr"] = o["d"] + lat + max([0.0] + [u["pr"] for u in users[o["i"]]])
     for o in ops:
         o["pr"] += o["up"]
-    free = {}
-    left = [len(o["deps"]) for o in ops]
-    cand = []
+    best = None
+    for _ in range(par["PASS"]):
+        seq = forward(ops, users, list(left), M, par["WIN"], cores, topo)
+        span = max(o["end"] for o in seq)
+        if best is None or span < best[0]:
+            best = (span, seq)
+        nxt = {}
+        for o in reversed(seq):
+            q = (o["r"], o["e"])
+            way = [o["end"] - o["t"]] + ([o["d"] + par["QW"] * nxt[q]] if q in nxt else [])
+            for u in users[o["i"]]:
+                if o["k"] == "r" and u["r"] != o["r"]:
+                    way.append(o["land"] - o["t"] + u["way"])
+                elif u["e"] == o["e"] and any(x is o for x in u["after"]):
+                    way.append(o["d"] + u["way"])
+                else:
+                    way.append(o["end"] - o["t"] + M["lat"] + u["way"])
+            o["way"] = nxt[q] = max(way)
+        for o in ops:
+            o["pr"] = par["MIX"] * o["pr"] + (1 - par["MIX"]) * (o["way"] + o["up"])
+    return best[1], total
 
-    def enter(o):
-        o["rdy"] = max([0.0] + [d["end"] + LAT for d in o["deps"]] + [x[2] + LAT for x in o["ext"]])
-        cand.append(o)
+
+def forward(ops, users, left, M, win, cores, topo):
+    S, seq = {}, []
     for o in ops:
-        if not o["deps"]:
-            enter(o)
-    seq = []
+        o["d"] = dur(o, M)
+    cand = [o for o in ops if not left[o["i"]]]
+    for o in cand:
+        o["rdy"] = 0.0
     while cand:
         for o in cand:
-            o["t"] = max(free.get(o["e"], 0.0), o["rdy"])
+            o["t"] = max(S.get((o["r"], o["e"]), 0.0), o["rdy"])
         first = min(cand, key=lambda o: (o["t"], -o["pr"]))
-        o = max([x for x in cand if x["e"] == first["e"] and x["t"] <= first["t"] + EST["win"]], key=lambda x: x["pr"])
-        cand[:] = [x for x in cand if x["i"] != o["i"]]
-        free[o["e"]] = o["t"] + o["d"]
-        o["end"] = o["t"] + o["d"] + o["lat"]
+        o = max([x for x in cand if x["e"] == first["e"] and x["r"] == first["r"] and x["t"] <= first["t"] + win[x["e"]]], key=lambda x: x["pr"])
+        cand = [x for x in cand if x is not o]
+        run(o, o["t"], S, M, cores, topo)
         seq.append(o)
         for u in users[o["i"]]:
             left[u["i"]] -= 1
-            if left[u["i"]] == 0:
-                enter(u)
-    return seq
-
-
-def landings(r, seq, T, topo, arr):
-    busy, first = {}, EST["first"]
-    for o in seq:
-        if o["k"] != "r":
-            continue
-        for (dst, src, a, b, mask, sem) in o["send"]:
-            far = topo.host(T.cores[dst]) != topo.host(T.cores[r])
-            rate = (EST["far"] if far else EST["near"]) * bits(mask)
-            t0 = o["t"] + o["d"] + first + 1500.0
-            es = [e for e in topo.engines(T.cores[r], T.cores[dst]) if mask >> e & 1]
-            t1 = max([t0] + [busy.get(e, 0.0) for e in es]) + 256.0 * (b - a) / rate
-            for e in es:
-                busy[e] = t1
-            old = arr.get((dst, sem), (0.0, 0))
-            arr[(dst, sem)] = (max(old[0], t1 + 500.0), old[1] + bits(mask))
-        first = 0.0
-
-
-def plan(rank, g, T, topo):
-    arr = {}
-    for r in range(NR - 1, rank - 1, -1):
-        seq = order(build(r, g, T, topo, arr))
-        landings(r, seq, T, topo, arr)
+            if not left[u["i"]]:
+                u["rdy"] = ready(u, S, M)
+                cand.append(u)
     return seq
 
 
@@ -364,25 +529,25 @@ def rank_program(g, core, T, topo):
     rank = T.rank_of(core)
     if rank is None:
         return
-    seq = plan(rank, g, T, topo)
+    seq, total = plan(T.cores, topo)
     Q = {"v": g.vector, "a": g.scalar, "p": g.tensor, "s": g.sync, "g": g}
     cnt = {e: 0 for e in CSEM}
     seen = {}
     sent = 0
     stores = []
     for o in seq:
+        if o["r"] != rank:
+            continue
         e = o["e"]
-        need = {}
+        need = {s: total[(rank, s)] for s in o["ext"]}
         for d in o["deps"]:
             s, v = d["sig"]
-            need[s] = max(need.get(s, 0), v)
-        for (s, v, _) in o["ext"]:
             need[s] = max(need.get(s, 0), v)
         for s, v in need.items():
             if seen.get((e, s), 0) < v:
                 Q[e].wait_ge(T.sem[s], v)
                 seen[(e, s)] = v
-        ins = o["fn"]()
+        ins = o["fn"](g, T)
         if o["k"] == "c":
             for x in ins:
                 x.then_inc(T.sem[CSEM[e]], 1)
@@ -394,7 +559,7 @@ def rank_program(g, core, T, topo):
             if o["sem"].startswith("st"):
                 stores.append(o["sem"])
         else:
-            sent += sum(bits(x[4]) for x in o["send"])
+            sent += sum(bits(x["mask"]) for x in o["send"])
     if sent:
         g.wait_ge(T.sem.sent, sent)
     for e in CSEM:

from concourse.bass import DstId, RemoteDMATransfer
from concourse.mybir import AluOpType as A, ActivationFunctionType as F

V, NR, CAP = 1792, 4, 192
L = NR * V
GAP = 16
TW = V + GAP
WW = NR * TW + 32
C, B = 0.0122, 3584.0
K = 1.0 / C
MAGIC = 12582912.0
ROOT = 3072.0
OB = 192.0
BIG = 8192.0
TOP = 200.0
Q4 = V // 4

PAR = {"LC":[96,320,320,608,448],"IC":[[[608,576,288,320],[480,352,416,544]],[[928,864],[288,288,672,544]],[[448,384,384,576],[384,352,224,288,544]],[[576,384,832],[672,192,192,352,352,32]]],"PT":[[[[384,176],[480,80],[320,48],[416,48],[192,64]],[[416,224],[448,144],[352,112],[192,64]]],[[[448,272],[448,32],[416,48],[320,0],[160,48]],[[352,128],[480,224],[-160,16,0],[-224,48,0],[448,80],[128,128]]],[[[224,128],[96,80],[512,80],[512,80],[288,112],[160,0]],[[160,160],[256,0],[352,176],[256,80],[-160,0,1],[-224,32,1],[256,16],[160,64]]],[[[96,96],[96,0],[64,0],[256,80],[320,96],[480,112],[480,0]],[[32,32],[448,160],[384,0],[128,64],[-352,32,2],[384,128],[96,96],[256,0],[64,0]]]],"EI":[["aav","aaa"],["vva","aav"],["vvv","aav"],["vvv","avv"]],"PC":[[[96,608,640,448],[96,608,640,448]],[[320,512,512,288,160],[544,256,224,768]]],"DUP":[[0,0],[2,3]],"PO":[[[],[800,800,192]],[[64,448,1280],[832,416,384,160]]],"ED":["axyxwvvvvv","xvayyxvvvv","wvavxwwyvv","avxxwayxwa"],"FO":[0,1,0,1],"RAW":[2,1,1,9],"PASS":1,"MIX":0.5,"QW":0.9,"LN":["gv","ga",None],"NAUX":3,"SPLIT":300,"UP":[{"i1a":-1000,"i1v":9000,"i1p":9000,"j1p":8000,"sndg":-3000,"m0p":8000,"exa":-8000,"j0p":-8000,"g0v":3000,"v":-8000},{"i1a":9000,"i1v":9000,"i1p":9000,"j1v":3000,"g0v":1000,"dv":-3000,"g1a":1000,"dp":-1000,"j0a":1000},{"i1a":8000,"g0a":-8000,"j1v":-8000,"exa":8000,"i1p":-8000,"i1v":-8000,"sndg":8000,"cvv":-3000,"j0a":8000,"j1a":8000,"i0v":3000},{"i1a":8000,"i0a":30000,"m1v":30000,"i1v":8000,"g1a":-3000,"j0v":-1000,"dv":8000,"sndg":1000,"m0v":3000,"j0p":-3000,"j1p":-8000,"i0p":-1000}],"WIN":{"a":200,"v":30,"p":30,"g":200,"s":500},"HOP":[700,1000,700,1000],"HUB":[[1,1],[0,1]]}
HM = 1024
NP = 8

SCRATCH = {
    "W0": ("sbuf", [128, WW], "bfloat16"), "W1": ("sbuf", [128, WW], "bfloat16"),
    "G": ("sbuf", [128, 4 * V], "bfloat16"),
    "E": ("sbuf", [128, V], "int32"), "X": ("sbuf", [128, V], "float32"), "Yl": ("sbuf", [128, HM], "float32"),
    "F": ("sbuf", [128, V], "bfloat16"), "Ln": ("sbuf", [128, 2 * Q4], "float32"),
    "Ob": ("sbuf", [128, 2 * Q4], "bfloat16"), "zb": ("sbuf", [128, 2 * Q4], "bfloat16"),
    "mb": ("sbuf", [128, 6 * Q4], "bfloat16"), "cb": ("sbuf", [128, 6 * Q4], "bfloat16"),
    "fb": ("sbuf", [128, 6 * Q4], "bfloat16"), "top": ("sbuf", [128, Q4], "bfloat16"),
    "off": ("sbuf", [128, 2 * Q4], "uint16"),
    "rt": ("sbuf", [128, 4], "int32"), "a4": ("sbuf", [128, 4], "int32"), "a15": ("sbuf", [128, 4], "int32"),
    "a12": ("sbuf", [128, 4], "int32"), "f12": ("sbuf", [128, 4], "float32"), "row": ("sbuf", [128, 4], "float32"),
    "rf": ("sbuf", [128, 4], "float32"),
    "A2": ("sbuf", [128, 128], "bfloat16"), "Di": ("sbuf", [128, 128], "bfloat16"),
    "S": ("sbuf", [128, 512], "bfloat16"), "S4": ("sbuf", [128, 512], "float32"),
    "Q": ("sbuf", [128, 512], "bfloat16"), "P": ("sbuf", [128, 512], "bfloat16"),
    "Ig": ("sbuf", [128, 128], "bfloat16"), "Im": ("sbuf", [128, 128], "bfloat16"), "Ik": ("sbuf", [128, 128], "float32"),
    "NB": ("sbuf", [128, 128], "bfloat16"), "NN": ("sbuf", [128, 128], "bfloat16"), "NU": ("sbuf", [128, 128], "bfloat16"),
    "ND": ("sbuf", [128, 128], "bfloat16"), "z0": ("sbuf", [128, 16], "float32"), "rt2": ("sbuf", [128, 512], "bfloat16"),
}
for _i in range(8):
    SCRATCH["ps%d" % _i] = ("psum", [128, 512], "float32")
for _i in (1, 2):
    SCRATCH.update({"Gh%d" % _i: ("sbuf", [128, 4 * HM], "bfloat16"), "Ph%d" % _i: ("sbuf", [128, 512], "bfloat16"),
                    "Fh%d" % _i: ("sbuf", [128, HM], "bfloat16"), "Xh%d" % _i: ("sbuf", [128, HM], "float32"),
                    "offh%d" % _i: ("sbuf", [128, Q4], "uint16")})

SEMAPHORES = ["cv", "ca", "cp", "cg", "sent", "a0", "a1", "lr", "h0", "h1", "h2", "t0", "t1", "t2"]
SEMAPHORES += ["ld%d" % i for i in range(NP)] + ["st%d" % i for i in range(2 * NP)] + ["y%d" % i for i in range(NP)]
SEMAPHORES += ["f%d_%d_%d" % (rd, s, p) for rd in range(2) for s in (2, 3) for p in range(NP)]

EST = {"cy": 1.0, "pe": 0.63, "lat": 80.0, "fix": 15.0, "ga": 1.45, "far": 12.0, "near": 18.0, "port": 100.0, "loc": 500.0,
       "first": 1300.0, "eng": 60.0, "call": 550.0, "tr": 80.0, "up": 1000.0, "wake": 400.0, "dma": 1250.0, "win": 30.0, "off": 500.0}
CSEM = {"v": "cv", "a": "ca", "p": "cp", "g": "cg"}


def starts(ws):
    out, x = [], 0
    for w in ws:
        out.append((x, x + w))
        x += w
    return out


def bits(m):
    return bin(m).count("1")


def build(r, cores, topo, ops, par):
    core = cores[r]
    qs = list(range(r + 1, NR))
    nq = len(qs)
    own = r * TW + GAP
    W = ["W0", "W1"]
    share = [{} for _ in range(NR)]
    H = [0] * NR
    for h in range(NR):
        for x in par["PT"][h][1]:
            if x[0] < 0:
                share[x[2]].setdefault(h, []).append((H[x[2]], H[x[2]] - x[0]))
                H[x[2]] -= x[0]
    ups = [h for h in range(r + 1, NR) if any(h in share[o] for o in range(r + 1))]
    naux = par["NAUX"]
    tails = {}

    def op(eng, cost, deps, fn, ext=(), kind="c", sem=None, send=None, lab="", line=None):
        o = {"r": r, "e": eng, "c": cost, "deps": [x for x in deps if x is not None], "fn": fn, "ext": list(ext), "k": kind,
             "sem": sem, "send": send, "i": len(ops), "lab": lab, "after": [tails[line]] if line in tails else [],
             "up": par["UP"][r].get(lab + eng, 0.0)}
        if line:
            tails[line] = o
        ops.append(o)
        return o

    def V1(n, deps, fn, **kw):
        return op("v", ("v", n), deps, lambda g, T: [fn(g.vector, T)], **kw)

    def A1(n, deps, fn, table=None, **kw):
        return op("a", ("a", n, table), deps, lambda g, T: [fn(g.scalar, T)], **kw)

    def G1(n, deps, fn):
        return op("g", ("g", n), deps, lambda g, T: [fn(g, T)])

    def P1(n, deps, fn, **kw):
        return op("p", ("p", n), deps, lambda g, T: fn(g.tensor, T), **kw)

    def over(lst, lo, hi):
        return [o for (a, b, o) in lst if a < hi and lo < b]

    def mms(pu, n, terms):
        return lambda t, T: [t.matmul(T[pu][:, 0:n], T[a][:, a0:a0 + 128], T[b][:, b0:b1:s], j == 0, j == len(terms) - 1) for j, (a, a0, b, b0, b1, s) in enumerate(terms)]

    lds = []
    for j, (x0, x1) in enumerate(starts(par["LC"])):
        q = "s" if j % 2 == 0 else "a"
        lds.append(op(q, ("d", 512 * (x1 - x0)), [], lambda g, T, x0=x0, x1=x1, q=q: [(g.sync if q == "s" else g.scalar).dma_start(T.E[:, x0:x1], T.ends[:, x0:x1])],
                      kind="d", sem="ld%d" % j, lab="ld", line="ld"))
    ldr = op("s", ("d", 2048), [], lambda g, T: [g.sync.dma_start(T.rt[:], T.rights[:])], kind="d", sem="lr", lab="ld", line="ld")

    g4 = G1(4, [], lambda g, T: g.iota(T.a4[:], [[0, 4]], 0, 1))
    gD = G1(128, [], lambda g, T: g.iota(T.Di[:], [[1, 128]], 0, -1, allow_small_or_imprecise_dtypes=True))
    c12 = V1(4, [g4], lambda v, T: v.tensor_scalar(T.a12[:], T.a4[:], 12, None, A.bitwise_and))
    cro = V1(4, [c12], lambda v, T: v.tensor_scalar(T.row[:], T.a12[:], 0.0, None, A.is_equal))
    cS, cS4 = [[V1(n, [gD, cro], lambda v, T, i=i, b=b: v.tensor_scalar(T[b][:, 128 * i:128 * i + 128], T.Di[:], 4.0 * i, T.row[:, 0:1], A.is_equal, A.mult))
                for i in range(4 if on else 0)] for (b, n, on) in (("S", 64, True), ("S4", 128, par["RAW"][r]))]
    cK = V1(128, [gD], lambda v, T: v.tensor_scalar(T.Ik[:], T.Di[:], 0.0, K, A.is_equal, A.mult))
    cnt = []
    if nq:
        gA = G1(128, [], lambda g, T: g.iota(T.A2[:], [[-16, 8], [0, 4], [-1, 4]], 0, 1, allow_small_or_imprecise_dtypes=True))
        cf2 = V1(4, [c12], lambda v, T: v.tensor_copy(T.f12[:], T.a12[:]))
        cNB = V1(64, [gA, cf2], lambda v, T: v.tensor_scalar(T.NB[:], T.A2[:], T.f12[:, 0:1], None, A.is_equal))
        cNN = V1(64, [gA, cf2], lambda v, T: v.tensor_scalar(T.NN[:], T.A2[:], T.f12[:, 0:1], -1.0, A.is_equal, A.mult))
        cNU = G1(128, [cNB], lambda g, T: g.affine_select(T.NU[:], T.NB[:], [[-1, 128]], A.is_gt, 0.0, 0, 1))
        cM = V1(64, [gD], lambda v, T: v.tensor_scalar(T.Im[:], T.Di[:], 0.0, -BIG, A.is_equal, A.mult))
        cG = V1(64, [gD], lambda v, T: v.tensor_scalar(T.Ig[:], T.Di[:], 0.0, float(GAP), A.is_equal, A.mult))
        cTop = V1(Q4 / 2, [], lambda v, T: v.memset(T.top[:], TOP))
        cND = V1(256, [cNU, cM], lambda v, T: v.tensor_tensor(T.ND[:], T.NU[:], T.Im[:], A.add))
        cnt = [cNN, cND, cG]
    c15 = V1(4, [g4], lambda v, T: v.tensor_scalar(T.a15[:], T.a4[:], 15, None, A.bitwise_and))
    cf = V1(8, [c15, ldr], lambda v, T: v.tensor_tensor(T.rf[:], T.rt[:], T.a15[:], A.subtract))
    cQ = [V1(64, [cf, gD], lambda v, T, b=b: v.tensor_scalar(T.Q[:, 128 * b:128 * b + 128], T.Di[:], T.rf[:, b:b + 1], None, A.is_equal)) for b in range(4)]
    cT = V1(256, cQ, lambda v, T: v.transpose(T.P[:], T.Q[:]))
    cR = V1(256, [], lambda v, T: v.memset(T.rt2[0:32, :], ROOT)) if "a" in par["ED"][r] else None
    cz = V1(16, [], lambda v, T: v.memset(T.z0[:], 0.0))
    gap = [A1(16, [cz], lambda a, T: a.activation(T.W0[:, own - GAP:own], T.z0[:], F.Exp, bias=-C * B, scale=C), table="exp", line="ld"),
           V1(16, [], lambda v, T: v.memset(T.W1[:, own - GAP:own], 0.0))]
    end = [V1(16, [], lambda v, T, rd=rd: v.memset(T[W[rd]][:, NR * TW:WW], 0.0)) for rd in range(2)]

    wr = [[], []]
    cvs = []
    for j, (x0, x1) in enumerate(starts(par["LC"])):
        cv = V1(x1 - x0, [lds[j]], lambda v, T, x0=x0, x1=x1: v.tensor_copy(T.X[:, x0:x1], T.E[:, x0:x1]), lab="cv")
        cvs.append((x0, x1, cv))
        wr[0].append((x0, x1, A1(x1 - x0, [cv, gap[0]], lambda a, T, x0=x0, x1=x1: a.activation(T.W0[:, own + x0:own + x1], T.X[:, x0:x1], F.Exp, bias=-C * B, scale=C), table="exp", lab="ex")))
    allexp = [o for (_, _, o) in wr[0]]

    st = {"bank": [None] * naux + [[]] * (8 - naux), "nm": 0, "nu": 0, "ns": 0}

    def aux():
        st["nu"] += 1
        return (st["nu"] - 1) % naux

    def lnop(n, deps, fn, lab):
        return A1(n, deps + allexp, fn, table="ln", lab=lab)

    def index(rd):
        fins, prev = [], None
        lab = "i%d" % rd
        eo, ef, ez = par["EI"][r][rd]
        for (x0, x1) in starts(par["IC"][r][rd]):
            n, k0 = (x1 - x0) // 4, x0 // 4
            lab = ("j%d" if x1 == V else "i%d") % rd
            lc = Q4 * rd + k0
            u = aux()
            pu = "ps%d" % u
            raw = rd == 0 and len(fins) < par["RAW"][r]
            if raw:
                lay = [("S4", 128 * i, "X", x0 + i, x1, 4) for i in range(4)]
                t = rel = P1(16 * max(64, n), over(cvs, x0, x1) + cS4 + [st["bank"][u]], mms(pu, n, lay), lab=lab)
                s0, b0, terms, cost = 1.0, 0.0, [], 0
                if nq:
                    raw = False
                    t = A1(n, [rel], lambda a, T, lc=lc, n=n, pu=pu: a.activation(T.Ln[:, lc:lc + n], T[pu][:, 0:n], F.Identity, bias=-C * B, scale=C), lab=lab)
                    s0, b0 = K, B
                    terms, cost = [("Ik", 0, "Ln", lc, lc + n, 1)], 4 * max(64, n)
            else:
                lay = [("S", 128 * i, W[rd], own + x0 + i, own + x1, 4) for i in range(4)]
                rel = P1(4 * max(64, n), over(wr[rd], x0, x1) + cS + [st["bank"][u]], mms(pu, n, lay), lab=lab)
                t = lnop(n, [rel], lambda a, T, lc=lc, n=n, pu=pu: a.activation(T.Ln[:, lc:lc + n], T[pu][:, 0:n], F.Ln), lab)
                s0, b0 = K, B
                terms, cost = [("Ik", 0, "Ln", lc, lc + n, 1)], 4 * max(64, n)
            deps = [t, cK]
            if r == 0:
                if ez == "v":
                    z = V1(n, [t], lambda v, T, lc=lc, n=n: v.tensor_scalar(T.zb[:, lc:lc + n], T.Ln[:, lc:lc + n], C * (0.5 - B), None, A.is_lt), lab=lab)
                else:
                    z = A1(n, [t], lambda a, T, lc=lc, n=n: a.activation(T.zb[:, lc:lc + n], T.Ln[:, lc:lc + n], F.Relu, bias=8.0 * (0.5 - B), scale=-8.0 * K), lab=lab)
                terms.append(("Im", 0, "zb", lc, lc + n, 1))
                cost += max(64, n)
                deps.append(z)
            if nq:
                mb = nq * lc
                sc0, bi0 = K / V, (B + 0.5) / V - 0.5 + OB
                if eo == "v":
                    o1 = V1(n, [t], lambda v, T, lc=lc, n=n: v.tensor_scalar(T.Ob[:, lc:lc + n], T.Ln[:, lc:lc + n], sc0, bi0, A.mult, A.add), lab=lab)
                else:
                    o1 = A1(n, [t], lambda a, T, lc=lc, n=n: a.activation(T.Ob[:, lc:lc + n], T.Ln[:, lc:lc + n], F.Identity, bias=bi0, scale=sc0), lab=lab)
                ms = [V1(n / 2, [o1], lambda v, T, lc=lc, n=n, a=mb + j * n, q=q: v.tensor_scalar(T.mb[:, a:a + n], T.Ob[:, lc:lc + n], OB + q, None, A.is_equal), lab=lab) for j, q in enumerate(qs)]
                sc = []
                for j in range(nq):
                    pa = None if prev is None else prev[0] + (j + 1) * prev[1] - 1
                    sc.append(V1(n / 2, [ms[j], cTop] + ([] if prev is None else [prev[2][j]]),
                                 lambda v, T, a=mb + j * n, n=n, pa=pa: v.tensor_tensor_scan(T.cb[:, a:a + n], T.mb[:, a:a + n], T.top[:, 0:n], 0.0 if pa is None else T.cb[:, pa:pa + 1], A.add, A.min), lab=lab))
                prev = (mb, n, sc)
                m = nq * n
                ca = P1(2 * max(64, m), sc + cnt, mms(pu, m, [("NN", 0, "cb", mb, mb + m, 1), ("ND", 0, "mb", mb, mb + m, 1)]), lab=lab)
                if ef == "v":
                    fl = V1(m, [ca], lambda v, T, mb=mb, m=m, pu=pu: v.tensor_scalar(T.fb[:, mb:mb + m], T[pu][:, 0:m], -BIG - CAP - 0.5, None, A.is_lt), lab=lab)
                else:
                    fl = A1(m, [ca], lambda a, T, mb=mb, m=m, pu=pu: a.activation(T.fb[:, mb:mb + m], T[pu][:, 0:m], F.Relu, bias=-BIG - CAP, scale=-1.0), lab=lab)
                deps.append(fl)
                terms += [("Ig", 0, "Ob", lc, lc + n, 1)] + [("Im", 0, "fb", mb + j * n, mb + j * n + n, 1) for j in range(nq)]
                cost += (nq + 1) * max(64, n)
                shift = b0 + GAP * (1 - OB) - r * TW
            else:
                shift = b0 + GAP * NR - r * TW
            um = rel if raw else P1(cost, deps, mms(pu, n, terms), lab=lab)
            fin = V1(n, [um], lambda v, T, lc=lc, n=n, pu=pu, shift=shift: v.tensor_scalar(T.off[:, lc:lc + n], T[pu][:, 0:n], MAGIC + shift, MAGIC, A.add, A.subtract), lab=lab)
            st["bank"][u] = fin
            fins.append((x0, x1, fin))
        return fins

    def arrivals(rd):
        hub = par["HUB"][rd]
        fs = ["f%d_%d_%d" % (rd, s, p) for s in (2, 3) if hub[s - 2] == r for p in range(len(par["PC"][rd][s - 2]))]
        return fs + ([] if r == 3 or (r == 1 and 0 not in hub) else ["a%d" % rd])

    def tr(dst, sb, s0, db, d0, w, size, mask, sem):
        return {"dst": dst, "sb": sb, "s0": s0, "db": db, "d0": d0, "w": w, "by": 128 * w * size, "mask": mask, "sem": sem}

    def snd(lst, deps, ext=(), line=None, lab="snd"):
        def fn(g, T):
            out = []
            for x in lst:
                rid, pid = topo.addr(cores[x["dst"]], core)
                out.append(RemoteDMATransfer(dst_ids=[DstId(rid=rid, pnc=pid)], dma_engine_mask=x["mask"], remote_sem=T.sem[x["sem"]],
                                             src=T[x["sb"]][:, x["s0"]:x["s0"] + x["w"]], dst=T[x["db"]][:, x["d0"]:x["d0"] + x["w"]]))
            return [g.remote_dma_fused(out, local_sem=T.sem.sent)]
        return op("g", ("r",), deps, fn, ext=ext, kind="r", send=lst, lab=lab, line=line)

    def msk(dst):
        return topo.mask(core, cores[dst])

    def half(m):
        en = [e for e in range(m.bit_length()) if m >> e & 1]
        lo = sum(1 << e for e in en[:len(en) // 2])
        return lo, m & ~lo

    def upmask(hs):
        m = msk(hs[0]) & ~(msk(1) if r == 2 else 0) if hs else 0
        return [m] if len(hs) == 1 else half(m)

    def store(deps, ext, src, x0, x1):
        st["ns"] += 1
        op("s", ("d", 512 * (x1 - x0)), deps, lambda g, T: [g.sync.dma_start(T.y[:, x0:x1], T[src][:, x0:x1])], ext=ext, kind="d", sem="st%d" % (st["ns"] - 1), lab="st")

    def main(rd, fins):
        res = []
        tbl = [o for (_, _, o) in wr[rd]] + [gap[rd], end[rd]]
        nx = {o: share[o][r][0][0] for o in range(r) if r in share[o]}
        nx[r] = H[r] if rd else 0
        for pn, part in enumerate(par["PT"][r][rd]):
            w, wv = part[:2]
            ed = par["ED"][r][pn]
            mine = w > 0
            w = abs(w)
            o = r if mine else part[2]
            x0 = nx[o]
            x1 = nx[o] = x0 + w
            Gb, Pb, Fb, Xb, ob = [n + ("" if mine else "h%d" % (r - o)) for n in ("G", "P", "F", "X", "off")]
            oc = Q4 * rd if mine else 0
            ext = arrivals(rd) + ([] if mine else ["h%d" % o] + ["t%d" % q for q in range(o, r)])
            deps = tbl + (over(fins, x0, x1) if mine else [])
            gs = []

            def win(T, a, b, o=o, ob=ob, oc=oc):
                return T[W[rd]][:, o * TW:WW].indirect(T[ob][:, oc + a // 4:oc + b // 4])
            if wv:
                gs.append(op("v", ("gv", 4 * wv), deps, lambda g, T, a=x0, b=x0 + wv, win=win, Gb=Gb: [g.vector.tensor_copy(T[Gb][:, 4 * a:4 * b], win(T, a, b))], ext=ext, lab="g%d" % rd, line=par["LN"][0]))
            if wv < w:
                gs.append(op("a", ("ga", 4 * (w - wv)), deps, lambda g, T, a=x0 + wv, b=x1, win=win, Gb=Gb: [g.scalar.activation(T[Gb][:, 4 * a:4 * b], win(T, a, b), F.Copy)], ext=ext, lab="g%d" % rd, line=par["LN"][1]))
            cut = [(x0, x1)] if w < par["SPLIT"] else [(x0, x0 + w // 2), (x0 + w // 2, x1)]
            prev = [None] * len(cut)
            c0 = o * TW + GAP
            for b in range(4):
                bk = naux + st["nm"] % (8 - naux)
                st["nm"] += 1
                pm = "ps%d" % bk
                mm = P1(max(64, w), gs + [cT if mine else None] + st["bank"][bk], mms(pm, w, [(Pb, 128 * b, Gb, 4 * x0 + b, 4 * x1, 4)]), lab="m%d" % rd)
                for h, (xa, xb) in enumerate(cut):
                    def mx(v, T, pm=pm, b=b, x0=x0, xa=xa, xb=xb, c0=c0, Fb=Fb):
                        dst = T.W1[:, c0 + xa:c0 + xb] if rd == 0 else T[Fb][:, xa:xb]
                        src = T[W[rd]][:, c0 + xa:c0 + xb] if b == 0 else dst
                        return v.tensor_tensor(dst, T[pm][:, xa - x0:xb - x0], src, A.max)
                    prev[h] = V1(xb - xa, [mm, prev[h]], mx, lab="m%d" % rd, line=par["LN"][2])
                st["bank"][bk] = list(prev)
            res += [(xa, xb, prev[h]) for h, (xa, xb) in enumerate(cut)]
            if rd:
                ln = lnop(w, prev, lambda a, T, x0=x0, x1=x1, Xb=Xb, Fb=Fb: a.activation(T[Xb][:, x0:x1], T[Fb][:, x0:x1], F.Ln), "d")
                u = aux() if ed in "va" else None
                pu = "ps%s" % u
                if u is None:
                    if ed in "xy":
                        d1 = A1(w, [ln], lambda a, T, x0=x0, x1=x1, Xb=Xb: a.activation(T[Xb][:, x0:x1], T[Xb][:, x0:x1], F.Identity, bias=MAGIC + B, scale=K), lab="d")
                    else:
                        d1 = V1(w, [ln], lambda v, T, x0=x0, x1=x1, Xb=Xb: v.tensor_scalar(T[Xb][:, x0:x1], T[Xb][:, x0:x1], K, MAGIC + B, A.mult, A.add), lab="d")
                    if ed == "y":
                        d2 = A1(w, [d1], lambda a, T, x0=x0, x1=x1, Xb=Xb: a.activation(T[Xb][:, x0:x1], T[Xb][:, x0:x1], F.Identity, bias=-MAGIC), lab="d")
                    else:
                        d2 = V1(w, [d1], lambda v, T, x0=x0, x1=x1, Xb=Xb: v.tensor_scalar(T[Xb][:, x0:x1], T[Xb][:, x0:x1], MAGIC, None, A.subtract), lab="d")
                elif ed == "v":
                    d1 = P1(4 * max(64, w), [ln, cK, st["bank"][u]], mms(pu, w, [("Ik", 0, Xb, x0, x1, 1)]), lab="d")
                    d2 = V1(w, [d1], lambda v, T, x0=x0, x1=x1, pu=pu, Xb=Xb: v.tensor_scalar(T[Xb][:, x0:x1], T[pu][:, 0:x1 - x0], MAGIC + B, MAGIC, A.add, A.subtract), lab="d")
                else:
                    d1 = P1(5 * max(64, w), [ln, cK, cR, st["bank"][u]], lambda t, T, x0=x0, x1=x1, pu=pu, Xb=Xb: [
                        t.matmul(T[pu][:, 0:x1 - x0], T.Ik[:], T[Xb][:, x0:x1], True, False),
                        t.matmul(T[pu][:, 0:x1 - x0], T.rt2[0:1, 0:128], T.rt2[0:1, 0:x1 - x0], False, True)], lab="d")
                    d2 = A1(w, [d1], lambda a, T, x0=x0, x1=x1, pu=pu, Xb=Xb: a.activation(T[Xb][:, x0:x1], T[pu][:, 0:x1 - x0], F.Identity, bias=B - ROOT * ROOT), lab="d")
                if u is not None:
                    st["bank"][u] = d2
                if mine:
                    store([d2], [], "X", x0, x1)
                else:
                    back = [x for h in sorted(share[o]) for x in share[o][h]].index((x0, x1))
                    snd([tr(o, Xb, x0, "Yl", x0, w, 4, msk(o), "y%d" % back)], [d2])
        return res

    def sends(rd, fins):
        def pieces(ws):
            return [(a - (GAP if a == 0 else 0), b) for (a, b) in starts(ws)]

        def tb(dst, src, a, b, mask, sem):
            c = src * TW + GAP + a
            return tr(dst, W[rd], c, W[rd], c, b - a, 2, mask, sem)
        hub = par["HUB"][rd]
        pcs = {s: pieces(par["PC"][rd][s - 2]) for s in (2, 3)}
        on = {s: pcs[s][:max(0, len(pcs[s]) - par["DUP"][rd][s - 2])] for s in (2, 3)}

        def own_piece(lst, a, b):
            deps = over(wr[rd], a, b) + [gap[rd]]
            if rd:
                lst = lst + [tb(h, r, a, b, m, "t%d" % r) for h, m in zip(ups, upmask(ups))]
            if rd and share[r] and b == V:
                n, hs = b - a, sorted(share[r])
                if par["FO"][r] and len(ups) == 1 and H[r] <= 4 * n <= V:
                    lst[-1]["mask"], m = half(lst[-1]["mask"])
                    return snd(lst + [tr(hs[0], "off", Q4, "offh%d" % (hs[0] - r), 0, n, 2, m, "h%d" % r)], deps + over(fins, 0, 4 * n), line="own")
                snd([tr(h, "off", Q4, "offh%d" % (h - r), 0, H[r] // 4, 2, m, "h%d" % r) for h, m in zip(hs, upmask(hs))], over(fins, 0, H[r]))
            if lst:
                snd(lst, deps, line="own")
        if r >= 2:
            far = msk(1)
            for p, (a, b) in enumerate(pcs[r]):
                if p >= len(on[r]):
                    lst = [tb(hub[r - 2], r, a, b, half(far)[0], "f%d_%d_%d" % (rd, r, p)), tb(1 - hub[r - 2], r, a, b, half(far)[1], "a%d" % rd)]
                else:
                    lst = [tb(hub[r - 2], r, a, b, far, "f%d_%d_%d" % (rd, r, p))]
                if r == 3:
                    lst.append(tb(2, r, a, b, msk(2) & ~far, "a%d" % rd))
                own_piece(lst, a, b)
        else:
            for (a, b) in pieces(par["PO"][r][rd]):
                own_piece([tb(0, 1, a, b, msk(0) & ~(msk(2) if rd and ups else 0), "a%d" % rd)] if r else [], a, b)
        if r < 2:
            lo, hi = half(msk(1 - r))
            both = [x for x, y in zip(on[2], on[3]) if x == y and hub == [r, r]]
            for (a, b) in both:
                p = on[2].index((a, b))
                snd([tb(1 - r, 2, a, b, lo, "a%d" % rd), tb(1 - r, 3, a, b, hi, "a%d" % rd)], [], ["f%d_2_%d" % (rd, p), "f%d_3_%d" % (rd, p)], line="on2")
            for s in (2, 3):
                for p, (a, b) in enumerate(on[s]):
                    if hub[s - 2] == r and (a, b) not in both:
                        snd([tb(1 - r, s, a, b, hi if rd and r else lo | hi, "a%d" % rd)], [], ["f%d_%d_%d" % (rd, s, p)], line="on%d" % s)

    sends(0, None)
    if H[r]:
        snd([tr(h, "P", 0, "Ph%d" % (h - r), 0, 512, 2, m, "h%d" % r) for h, m in zip(sorted(share[r]), upmask(sorted(share[r])))], [cT])
    f0 = index(0)
    wr[1] = main(0, f0)
    f1 = index(1)
    sends(1, f1)
    for j, (x0, x1) in enumerate([x for h in sorted(share[r]) for x in share[r][h]]):
        store([], ["y%d" % j], "Yl", x0, x1)
    main(1, f1)


def dur(o, M):
    c = o["c"]
    k = c[0]
    if k == "v":
        return max(64.0, c[1]) * M["cy"] + M["fix"]
    if k == "a":
        return max(64.0, c[1]) * M["cy"] + M["fix"] + 20
    if k == "gv" or k == "ga":
        return c[1] * M["ga"] * M["cy"] + (50 if k == "gv" else 65)
    if k == "p":
        return c[1] * M["pe"] + M["fix"]
    if k == "g":
        return 170 + 2 * c[1] * M["cy"]
    return M["call"] + M["tr"] * len(o["send"]) if k == "r" else 60.0


def run(o, t, S, M, cores, topo):
    r = o["r"]
    o["t"] = t
    if o["c"][0] == "a" and o["c"][2] and S.get(("table", r)) != o["c"][2]:
        S[("table", r)] = o["c"][2]
        o["d"] += 1400.0
    o["end"] = S[(r, o["e"])] = t + o["d"]
    if o["k"] == "d":
        t1 = max([o["end"] + M["dma"]] + [S.get((r, e), 0.0) for e in range(16)]) + o["c"][1] / M["loc"]
        for e in range(16):
            S[(r, e)] = t1
        o["end"] = t1
    if o["k"] == "r":
        new = [e for x in o["send"] for e in range(16) if x["mask"] >> e & 1 and ("u", r, e) not in S]
        t0 = o["end"] + M["up"] + M["eng"] * len(new) + (0.0 if ("u", r) in S else M["first"])
        S[("u", r)] = 1
        for x in o["send"]:
            far = topo.host(cores[x["dst"]]) != topo.host(cores[r])
            es = [e for e in range(16) if x["mask"] >> e & 1]
            t1 = max([t0 + (M["off"] if far else 0.0)] + [S.get((r, e), 0.0) for e in es]) + x["by"] / ((M["far"] if far else M["near"]) * len(es))
            if far:
                S[("port", r)] = max(t0, S.get(("port", r), 0.0)) + x["by"] / M["port"]
                t1 = max(t1, S[("port", r)])
            for e in es:
                S[(r, e)] = t1
                S[("u", r, e)] = 1
            key = ("land", x["dst"], x["sem"])
            S[key] = max(S.get(key, 0.0), t1 + M["wake"])
            o["land"] = t1 + M["wake"]


def ready(o, S, M):
    return max([0.0] + [d["t"] for d in o["after"]] + [d["end"] + M["lat"] for d in o["deps"]] + [S[("land", o["r"], s)] for s in o["ext"]])


def plan(cores, topo, par=PAR, M=EST):
    ops = []
    for r in range(NR):
        build(r, cores, topo, ops, par)
    src, total = {}, {}
    for o in ops:
        o["d"] = dur(o, M)
        for x in o["send"] or []:
            src.setdefault((x["dst"], x["sem"]), []).append(o)
            total[(x["dst"], x["sem"])] = total.get((x["dst"], x["sem"]), 0) + bits(x["mask"])
    users = [[] for _ in ops]
    left = []
    for o in ops:
        pre = {d["i"] for d in o["deps"] + o["after"]} | {d["i"] for s in o["ext"] for d in src[(o["r"], s)]}
        left.append(len(pre))
        for i in pre:
            users[i].append(o)
    n, chain = list(left), [o for o in ops if not left[o["i"]]]
    for o in chain:
        for u in users[o["i"]]:
            n[u["i"]] -= 1
            if not n[u["i"]]:
                chain.append(u)
    for o in reversed(chain):
        lat = M["lat"]
        if o["k"] == "d":
            lat += M["dma"] + o["c"][1] / M["loc"]
        if o["k"] == "r":
            lat += M["up"] + M["wake"] + o["send"][0]["by"] / M["port"]
        if o["lab"] in ("i0", "i1"):
            lat += par["HOP"][o["r"]]
        o["pr"] = o["d"] + lat + max([0.0] + [u["pr"] for u in users[o["i"]]])
    for o in ops:
        o["pr"] += o["up"]
    best = None
    for _ in range(par["PASS"]):
        seq = forward(ops, users, list(left), M, par["WIN"], cores, topo)
        span = max(o["end"] for o in seq)
        if best is None or span < best[0]:
            best = (span, seq)
        nxt = {}
        for o in reversed(seq):
            q = (o["r"], o["e"])
            way = [o["end"] - o["t"]] + ([o["d"] + par["QW"] * nxt[q]] if q in nxt else [])
            for u in users[o["i"]]:
                if o["k"] == "r" and u["r"] != o["r"]:
                    way.append(o["land"] - o["t"] + u["way"])
                elif u["e"] == o["e"] and any(x is o for x in u["after"]):
                    way.append(o["d"] + u["way"])
                else:
                    way.append(o["end"] - o["t"] + M["lat"] + u["way"])
            o["way"] = nxt[q] = max(way)
        for o in ops:
            o["pr"] = par["MIX"] * o["pr"] + (1 - par["MIX"]) * (o["way"] + o["up"])
    return best[1], total


def forward(ops, users, left, M, win, cores, topo):
    S, seq = {}, []
    for o in ops:
        o["d"] = dur(o, M)
    cand = [o for o in ops if not left[o["i"]]]
    for o in cand:
        o["rdy"] = 0.0
    while cand:
        for o in cand:
            o["t"] = max(S.get((o["r"], o["e"]), 0.0), o["rdy"])
        first = min(cand, key=lambda o: (o["t"], -o["pr"]))
        o = max([x for x in cand if x["e"] == first["e"] and x["r"] == first["r"] and x["t"] <= first["t"] + win[x["e"]]], key=lambda x: x["pr"])
        cand = [x for x in cand if x is not o]
        run(o, o["t"], S, M, cores, topo)
        seq.append(o)
        for u in users[o["i"]]:
            left[u["i"]] -= 1
            if not left[u["i"]]:
                u["rdy"] = ready(u, S, M)
                cand.append(u)
    return seq


def rank_program(g, core, T, topo):
    rank = T.rank_of(core)
    if rank is None:
        return
    seq, total = plan(T.cores, topo)
    Q = {"v": g.vector, "a": g.scalar, "p": g.tensor, "s": g.sync, "g": g}
    cnt = {e: 0 for e in CSEM}
    seen = {}
    sent = 0
    stores = []
    for o in seq:
        if o["r"] != rank:
            continue
        e = o["e"]
        need = {s: total[(rank, s)] for s in o["ext"]}
        for d in o["deps"]:
            s, v = d["sig"]
            need[s] = max(need.get(s, 0), v)
        for s, v in need.items():
            if seen.get((e, s), 0) < v:
                Q[e].wait_ge(T.sem[s], v)
                seen[(e, s)] = v
        ins = o["fn"](g, T)
        if o["k"] == "c":
            for x in ins:
                x.then_inc(T.sem[CSEM[e]], 1)
                cnt[e] += 1
            o["sig"] = (CSEM[e], cnt[e])
        elif o["k"] == "d":
            ins[0].then_inc(T.sem[o["sem"]], 16)
            o["sig"] = (o["sem"], 16)
            if o["sem"].startswith("st"):
                stores.append(o["sem"])
        else:
            sent += sum(bits(x["mask"]) for x in o["send"])
    if sent:
        g.wait_ge(T.sem.sent, sent)
    for e in CSEM:
        if max([0] + [v for (k, v) in seen.items() if k[1] == CSEM[e]]) < cnt[e]:
            g.wait_ge(T.sem[CSEM[e]], cnt[e])
    for s in stores:
        g.sync.wait_ge(T.sem[s], 16)
